import numpy as np
import ml_dtypes


def mxq(x, axis, fmt="e4m3"):
    dtype, down = {"e4m3": (ml_dtypes.float8_e4m3fn, 7), "e5m2": (ml_dtypes.float8_e5m2, 14)}[fmt]
    v = np.moveaxis(np.asarray(x, np.float32).astype(ml_dtypes.bfloat16).astype(np.float64), axis, -1)
    blocks = v.reshape(v.shape[:-1] + (-1, 32))
    amax = np.abs(blocks).max(-1, keepdims=True)
    byte = np.maximum(np.where(amax > 0, np.frexp(amax)[1] - 1 + 127, 0) - down, 1)
    scale = np.exp2(byte - 127.0)
    codes = (blocks / scale).astype(np.float32).astype(dtype).astype(np.float64)
    return np.moveaxis((codes * scale).reshape(v.shape), -1, axis)


WIDE = False


def mx_kscale(k):
    if not WIDE:
        return np.ones(k)
    levels = np.array([10, -10, 5, -5, 0])
    if k % 512:
        return np.exp2(np.random.permutation(np.resize(levels, k // 32))).repeat(32)
    a = np.empty((k // 512, 16))
    for p in range(k // 512):
        a[p, :8] = np.random.permutation(np.resize(levels, 8))
        for g in range(8):
            far = levels[np.abs(levels - a[p, g]) >= 10]
            a[p, g + 8] = far[np.random.randint(len(far))]
    return np.exp2(a.ravel()).repeat(32)


def f64(x):
    return np.asarray(x).astype(np.float64)


def striped(idx):
    return np.tile(np.asarray(idx).reshape(-1, 16).T, (8, 1)).astype(np.uint16)


def unstriped(offs):
    return offs[:16].T.reshape(-1).astype(np.int64)

def rot(x):
    y = x.reshape(x.shape[0], -1, 2, x.shape[2])
    return np.stack([-y[:, :, 1], y[:, :, 0]], axis=2).reshape(x.shape)


B, N, T, D, NQ = 1, 512, 2048, 512, 128


def setup_inputs():
    n = np.random.standard_normal
    idx = np.random.permutation(T)[:B * N]
    idx2 = np.random.permutation(1024)[:B * N]
    s = mx_kscale(D)[:, None]
    return {
        "qT": (n((B, D, NQ)) * s * (1.00 / np.sqrt(D))).astype(np.float32),
        "kT": (np.clip(np.round(n((D, T)) * 16), -64, 64) / 16 / s).astype(np.float32),
        "cT": (np.repeat(np.round(np.cos(np.arange(D // 2)[:, None] * 0.11 + np.arange(1024)[None] * 0.37) * 64) / 64, 2, axis=0)).astype(np.float32),
        "wT": (np.repeat(np.round(np.sin(np.arange(D // 2)[:, None] * 0.11 + np.arange(1024)[None] * 0.37) * 64) / 64, 2, axis=0)).astype(np.float32),
        "kb": np.tile(n(2048), (128, 1)).astype(np.float32),
        "offs": striped(idx),
        "offs2": striped(idx2),
    }


def reference(qT, kT, cT, wT, kb, offs, offs2):
    idx = unstriped(offs)
    idx2 = unstriped(offs2)
    pick = lambda x, which: x[:, which].reshape(x.shape[0], B, -1).transpose(1, 0, 2)
    kg = pick(f64(kT), idx)
    cg = pick(f64(cT), idx2)
    wg = pick(f64(wT), idx2)
    ug = mxq(kg * cg + rot(kg) * wg, 1, "e4m3")
    qq = mxq(f64(qT), 1, "e4m3")
    a = qq.transpose(0, 2, 1) @ ug
    x = a + pick(f64(kb), idx)[:, :1, :]
    m = np.max(x, axis=-1, keepdims=True)
    e = np.exp(x - m)
    y = e / np.sum(e, axis=-1, keepdims=True)
    return y

@@ -1,0 +1,165 @@
+from contextlib import ExitStack
+
+import concourse.mybir as mybir
+from concourse.masks import make_identity
+
+N, T, T2, D, NQ = 512, 2048, 1024, 512, 128
+FLOPS = 2 * NQ * N * D
+BYTES = 4 * (D * NQ + D * T + 2 * D * T2 + T + NQ * N) + 2 * 2 * 128 * (N // 16)
+
+F32 = mybir.dt.float32
+BF16 = mybir.dt.bfloat16
+U32 = mybir.dt.uint32
+U16 = mybir.dt.uint16
+U8 = mybir.dt.uint8
+FP8X4 = mybir.dt.float8_e4m3fn_x4
+ALU = mybir.AluOpType
+ACT = mybir.ActivationFunctionType
+AX = mybir.AxisListType
+
+P = 128
+PACK = 4
+CHUNKS = 2
+CW = N // CHUNKS
+
+
+def tile_attend_pre_ropew_f_topk_kernel(tc, qT, kT, cT, wT, kb, offs, offs2, out):
+    nc = tc.nc
+    with ExitStack() as ctx:
+        pool = ctx.enter_context(tc.tile_pool(name="held", bufs=1))
+        psum = ctx.enter_context(tc.psum_pool(name="psum", bufs=1))
+
+        tok = pool.tile([P, N // 16], U16, name="tok")
+        pos = pool.tile([P, N // 16], U16, name="pos")
+        k_win = [pool.tile([P, T], F32, name="k_win%d" % t) for t in range(PACK)]
+        c_win = [pool.tile([P, T2], F32, name="c_win%d" % t) for t in range(PACK)]
+        w_win = [pool.tile([P, T2], F32, name="w_win%d" % t) for t in range(PACK)]
+        b_win = pool.tile([P, T], F32, name="b_win")
+        q_raw = pool.tile([P, PACK, NQ], F32, name="q_raw")
+
+        k_rows = kT.rearrange("(p t) n -> t p n", t=PACK)
+        c_rows = cT.rearrange("(p t) n -> t p n", t=PACK)
+        w_rows = wT.rearrange("(p t) n -> t p n", t=PACK)
+
+        warm = pool.tile([P, 8], F32, name="warm")
+        warm_out = pool.tile([P, 8], F32, name="warm_out")
+        nc.gpsimd.memset(warm[:], 0.0)
+        nc.scalar.activation(warm_out[:], warm[:], ACT.Exp)
+
+        nc.sync.dma_start(tok[:], offs)
+        nc.sync.dma_start(k_win[0][:], k_rows[0])
+        nc.sync.dma_start(pos[:], offs2)
+        nc.vector.memset(b_win[:], 0.0)
+        nc.scalar.dma_start(b_win[0:1, :], kb[0:1, :])
+        ident = pool.tile([P, P], F32, name="ident")
+        make_identity(nc, ident[:])
+        for even in (0, 2):
+            odd = even + 1
+            if even:
+                nc.sync.dma_start(k_win[even][:], k_rows[even])
+            nc.sync.dma_start(c_win[even][:], c_rows[even])
+            nc.sync.dma_start(w_win[odd][:], w_rows[odd])
+            nc.sync.dma_start(k_win[odd][:], k_rows[odd])
+            nc.sync.dma_start(c_win[odd][:], c_rows[odd])
+            nc.sync.dma_start(w_win[even][:], w_rows[even])
+        nc.sync.dma_start(q_raw[:], qT[0].rearrange("(p t) m -> p t m", t=PACK))
+
+        kg = pool.tile([P, PACK, N], F32, name="kg")
+        neg_kg = pool.tile([P, 2, N], F32, name="neg_kg")
+        kc = pool.tile([P, PACK, N], F32, name="kc")
+        kw = pool.tile([P, PACK, N], F32, name="kw")
+        u_bf = pool.tile([P, N, PACK], BF16, name="u_bf", align_bytes=64)
+        bg = pool.tile([P, N], F32, name="bg")
+        b_col = pool.tile([P, N // P], F32, name="b_col")
+        neg_b = pool.tile([P, N], F32, name="neg_b")
+
+        def add_pair(even, cols):
+            nc.vector.tensor_tensor(
+                u_bf[:, cols, even : even + 2],
+                kc[:, even : even + 2, cols].rearrange("p t n -> p n t"),
+                kw[:, even : even + 2, cols].rearrange("p t n -> p n t"),
+                ALU.add,
+            )
+
+        def bias_rows():
+            nc.vector.tensor_copy(bg[:], b_win[:].indirect(tok[:]))
+            turned = psum.tile([P, N // P, P], F32, name="turned")
+            for c in range(N // P):
+                nc.tensor.transpose(turned[:, c, :], bg[:, c * P : (c + 1) * P], ident[:])
+            nc.scalar.activation(b_col[:], turned[:, :, 0], ACT.Copy, scale=-1.0)
+            spread = psum.tile([P, N], F32, name="spread")
+            for c in range(N // P):
+                nc.tensor.transpose(
+                    spread[:, c * P : (c + 1) * P], b_col[:, c : c + 1].to_broadcast([P, P]), ident[:]
+                )
+            nc.scalar.copy(neg_b[:], spread[:])
+
+        for even in (0, 2):
+            odd = even + 1
+            nc.vector.tensor_copy(kg[:, even, :], k_win[even][:].indirect(tok[:]))
+            nc.vector.tensor_tensor(kc[:, even, :], c_win[even][:].indirect(pos[:]), kg[:, even, :], ALU.mult)
+            nc.vector.tensor_tensor(kw[:, odd, :], w_win[odd][:].indirect(pos[:]), kg[:, even, :], ALU.mult)
+            if even == 0:
+                bias_rows()
+            nc.vector.tensor_copy(kg[:, odd, :], k_win[odd][:].indirect(tok[:]))
+            nc.scalar.activation(neg_kg[:, even // 2, :], kg[:, odd, :], ACT.Copy, scale=-1.0)
+            nc.vector.tensor_tensor(kc[:, odd, :], c_win[odd][:].indirect(pos[:]), kg[:, odd, :], ALU.mult)
+            if even == 0:
+                nc.vector.tensor_tensor(kw[:, 0, :], w_win[0][:].indirect(pos[:]), neg_kg[:, 0, :], ALU.mult)
+                add_pair(0, slice(0, N))
+
+        chunks = [slice(c * CW, (c + 1) * CW) for c in range(CHUNKS)]
+        for c, cols in enumerate(chunks):
+            lst = pos[:, c * (CW // 16) : (c + 1) * (CW // 16)]
+            nc.vector.tensor_tensor(kw[:, 2, cols], w_win[2][:].indirect(lst), neg_kg[:, 1, cols], ALU.mult)
+
+        q_bf = pool.tile([P, NQ, PACK], BF16, name="q_bf", align_bytes=64)
+        q_codes = pool.tile([P, NQ], U32, name="q_codes", align_bytes=64)
+        q_scales = pool.tile([P, NQ], U8, name="q_scales", align_bytes=64)
+        nc.scalar.copy(q_bf[:], q_raw[:].rearrange("p t m -> p m t"))
+
+        add_pair(2, chunks[0])
+        nc.vector.quantize_mx(
+            out=q_codes[:].bitcast(FP8X4), scales=q_scales[:], in_=q_bf[:].rearrange("p m t -> p (m t)")
+        )
+        u_codes = [pool.tile([P, CW], U32, name="u_codes%d" % c, align_bytes=64) for c in range(CHUNKS)]
+        u_scales = [pool.tile([P, CW], U8, name="u_scales%d" % c, align_bytes=64) for c in range(CHUNKS)]
+        scores = [psum.tile([P, CW], F32, name="scores%d" % c) for c in range(CHUNKS)]
+        neg_x = pool.tile([P, N], F32, name="neg_x")
+
+        def score(c):
+            nc.vector.quantize_mx(
+                out=u_codes[c][:].bitcast(FP8X4),
+                scales=u_scales[c][:],
+                in_=u_bf[:, chunks[c], :].rearrange("p n t -> p (n t)"),
+            )
+            nc.tensor.matmul_mx(
+                out=scores[c][:],
+                lhsT=q_codes[:].bitcast(FP8X4),
+                lhsT_scale=q_scales[:],
+                rhs=u_codes[c][:].bitcast(FP8X4),
+                rhs_scale=u_scales[c][:],
+                start=True,
+                stop=True,
+            )
+
+        score(0)
+        add_pair(2, chunks[1])
+        nc.vector.tensor_tensor(neg_x[:, chunks[0]], neg_b[:, chunks[0]], scores[0][:], ALU.subtract)
+        score(1)
+        first_min = pool.tile([P, 1], F32, name="first_min")
+        nc.vector.tensor_reduce(first_min[:], neg_x[:, chunks[0]], AX.X, ALU.min)
+        nc.vector.tensor_tensor(neg_x[:, chunks[1]], neg_b[:, chunks[1]], scores[1][:], ALU.subtract)
+        neg_m = pool.tile([P, 1], F32, name="neg_m")
+        spare = pool.tile([P, CW], F32, name="spare")
+        nc.vector.tensor_scalar(
+            spare[:], neg_x[:, chunks[1]], 1.0, first_min[:], ALU.mult, ALU.min, accum_out=neg_m[:]
+        )
+        e = pool.tile([P, N], F32, name="e")
+        total = pool.tile([P, 1], F32, name="total")
+        nc.scalar.activation(e[:], neg_x[:], ACT.Exp, bias=neg_m[:], scale=-1.0, accum_out=total[:])
+        inv = pool.tile([P, 1], F32, name="inv")
+        nc.vector.reciprocal(inv[:], total[:])
+        y = pool.tile([P, N], F32, name="y")
+        nc.vector.tensor_scalar_mul(y[:], e[:], inv[:])
+        nc.sync.dma_start(out[0], y[:])

@@ -19,8 +19,7 @@ AX = mybir.AxisListType
 
 P = 128
 PACK = 4
-CHUNKS = 2
-CW = N // CHUNKS
+WIDTHS = (128, 128, 128, 128)
 
 
 def tile_attend_pre_ropew_f_topk_kernel(tc, qT, kT, cT, wT, kb, offs, offs2, out):
@@ -47,10 +46,10 @@ def tile_attend_pre_ropew_f_topk_kernel(tc, qT, kT, cT, wT, kb, offs, offs2, out
         nc.scalar.activation(warm_out[:], warm[:], ACT.Exp)
 
         nc.sync.dma_start(tok[:], offs)
+        nc.sync.dma_start(b_win[P - 1 : P, :], kb[0:1, :])
         nc.sync.dma_start(k_win[0][:], k_rows[0])
         nc.sync.dma_start(pos[:], offs2)
-        nc.vector.memset(b_win[:], 0.0)
-        nc.scalar.dma_start(b_win[0:1, :], kb[0:1, :])
+        nc.vector.memset(b_win[0 : P - 1, :], 0.0)
         ident = pool.tile([P, P], F32, name="ident")
         make_identity(nc, ident[:])
         for even in (0, 2):
@@ -58,8 +57,8 @@ def tile_attend_pre_ropew_f_topk_kernel(tc, qT, kT, cT, wT, kb, offs, offs2, out
             if even:
                 nc.sync.dma_start(k_win[even][:], k_rows[even])
             nc.sync.dma_start(c_win[even][:], c_rows[even])
-            nc.sync.dma_start(w_win[odd][:], w_rows[odd])
             nc.sync.dma_start(k_win[odd][:], k_rows[odd])
+            nc.sync.dma_start(w_win[odd][:], w_rows[odd])
             nc.sync.dma_start(c_win[odd][:], c_rows[odd])
             nc.sync.dma_start(w_win[even][:], w_rows[even])
         nc.sync.dma_start(q_raw[:], qT[0].rearrange("(p t) m -> p t m", t=PACK))
@@ -68,98 +67,130 @@ def tile_attend_pre_ropew_f_topk_kernel(tc, qT, kT, cT, wT, kb, offs, offs2, out
         neg_kg = pool.tile([P, 2, N], F32, name="neg_kg")
         kc = pool.tile([P, PACK, N], F32, name="kc")
         kw = pool.tile([P, PACK, N], F32, name="kw")
+        u_pair = pool.tile([P, 2, N, 2], BF16, name="u_pair", align_bytes=64)
         u_bf = pool.tile([P, N, PACK], BF16, name="u_bf", align_bytes=64)
         bg = pool.tile([P, N], F32, name="bg")
         b_col = pool.tile([P, N // P], F32, name="b_col")
         neg_b = pool.tile([P, N], F32, name="neg_b")
+        pair_words = u_pair[:].rearrange("p h n e -> p (h n e)").bitcast(F32).rearrange("p (h n) -> p n h", h=2)
+        u_words = u_bf[:].rearrange("p n t -> p (n t)").bitcast(F32).rearrange("p (n h) -> p n h", h=2)
 
         def add_pair(even, cols):
             nc.vector.tensor_tensor(
-                u_bf[:, cols, even : even + 2],
+                u_pair[:, even // 2, cols, :],
                 kc[:, even : even + 2, cols].rearrange("p t n -> p n t"),
                 kw[:, even : even + 2, cols].rearrange("p t n -> p n t"),
                 ALU.add,
             )
 
-        def bias_rows():
-            nc.vector.tensor_copy(bg[:], b_win[:].indirect(tok[:]))
-            turned = psum.tile([P, N // P, P], F32, name="turned")
-            for c in range(N // P):
-                nc.tensor.transpose(turned[:, c, :], bg[:, c * P : (c + 1) * P], ident[:])
-            nc.scalar.activation(b_col[:], turned[:, :, 0], ACT.Copy, scale=-1.0)
-            spread = psum.tile([P, N], F32, name="spread")
-            for c in range(N // P):
-                nc.tensor.transpose(
-                    spread[:, c * P : (c + 1) * P], b_col[:, c : c + 1].to_broadcast([P, P]), ident[:]
-                )
-            nc.scalar.copy(neg_b[:], spread[:])
+        nc.vector.tensor_copy(bg[:], b_win[:].indirect(tok[:]))
+        turned = psum.tile([P, N // P, P], F32, name="turned")
+        for c in range(N // P):
+            nc.tensor.transpose(turned[:, c, :], bg[:, c * P : (c + 1) * P], ident[:])
+        nc.scalar.activation(b_col[:], turned[:, :, P - 1], ACT.Copy, scale=-1.0)
+        spread = psum.tile([P, N], F32, name="spread")
+        for c in range(N // P):
+            nc.tensor.transpose(spread[:, c * P : (c + 1) * P], b_col[:, c : c + 1].to_broadcast([P, P]), ident[:])
+        nc.scalar.copy(neg_b[:], spread[:])
 
         for even in (0, 2):
             odd = even + 1
+            if even:
+                add_pair(0, slice(0, N // 2))
             nc.vector.tensor_copy(kg[:, even, :], k_win[even][:].indirect(tok[:]))
+            if even:
+                add_pair(0, slice(N // 2, N))
             nc.vector.tensor_tensor(kc[:, even, :], c_win[even][:].indirect(pos[:]), kg[:, even, :], ALU.mult)
-            nc.vector.tensor_tensor(kw[:, odd, :], w_win[odd][:].indirect(pos[:]), kg[:, even, :], ALU.mult)
-            if even == 0:
-                bias_rows()
             nc.vector.tensor_copy(kg[:, odd, :], k_win[odd][:].indirect(tok[:]))
             nc.scalar.activation(neg_kg[:, even // 2, :], kg[:, odd, :], ACT.Copy, scale=-1.0)
+            nc.vector.tensor_tensor(kw[:, odd, :], w_win[odd][:].indirect(pos[:]), kg[:, even, :], ALU.mult)
             nc.vector.tensor_tensor(kc[:, odd, :], c_win[odd][:].indirect(pos[:]), kg[:, odd, :], ALU.mult)
             if even == 0:
                 nc.vector.tensor_tensor(kw[:, 0, :], w_win[0][:].indirect(pos[:]), neg_kg[:, 0, :], ALU.mult)
-                add_pair(0, slice(0, N))
-
-        chunks = [slice(c * CW, (c + 1) * CW) for c in range(CHUNKS)]
-        for c, cols in enumerate(chunks):
-            lst = pos[:, c * (CW // 16) : (c + 1) * (CW // 16)]
-            nc.vector.tensor_tensor(kw[:, 2, cols], w_win[2][:].indirect(lst), neg_kg[:, 1, cols], ALU.mult)
 
         q_bf = pool.tile([P, NQ, PACK], BF16, name="q_bf", align_bytes=64)
         q_codes = pool.tile([P, NQ], U32, name="q_codes", align_bytes=64)
         q_scales = pool.tile([P, NQ], U8, name="q_scales", align_bytes=64)
-        nc.scalar.copy(q_bf[:], q_raw[:].rearrange("p t m -> p m t"))
-
-        add_pair(2, chunks[0])
-        nc.vector.quantize_mx(
-            out=q_codes[:].bitcast(FP8X4), scales=q_scales[:], in_=q_bf[:].rearrange("p m t -> p (m t)")
-        )
-        u_codes = [pool.tile([P, CW], U32, name="u_codes%d" % c, align_bytes=64) for c in range(CHUNKS)]
-        u_scales = [pool.tile([P, CW], U8, name="u_scales%d" % c, align_bytes=64) for c in range(CHUNKS)]
-        scores = [psum.tile([P, CW], F32, name="scores%d" % c) for c in range(CHUNKS)]
+        u_codes = pool.tile([P, N], U32, name="u_codes", align_bytes=64)
+        u_scales = pool.tile([P, N], U8, name="u_scales", align_bytes=64)
+        chunks = []
+        for w in WIDTHS:
+            first = chunks[-1].stop if chunks else 0
+            chunks.append(slice(first, first + w))
+        scores = [psum.tile([P, w], F32, name="scores%d" % c) for c, w in enumerate(WIDTHS)]
         neg_x = pool.tile([P, N], F32, name="neg_x")
+        mins = [pool.tile([P, 1], F32, name="min%d" % c) for c in range(len(WIDTHS))]
+        spare = pool.tile([P, N], F32, name="spare")
+
+        def last_gather(c):
+            cols = chunks[c]
+            lst = pos[:, cols.start // 16 : cols.stop // 16]
+            nc.vector.tensor_tensor(kw[:, 2, cols], w_win[2][:].indirect(lst), neg_kg[:, 1, cols], ALU.mult)
+
+        def join(c):
+            add_pair(2, chunks[c])
+            nc.scalar.copy(u_words[:, chunks[c], :], pair_words[:, chunks[c], :])
 
         def score(c):
+            cols = chunks[c]
             nc.vector.quantize_mx(
-                out=u_codes[c][:].bitcast(FP8X4),
-                scales=u_scales[c][:],
-                in_=u_bf[:, chunks[c], :].rearrange("p n t -> p (n t)"),
+                out=u_codes[:, cols].bitcast(FP8X4),
+                scales=u_scales[:, cols],
+                in_=u_bf[:, cols, :].rearrange("p n t -> p (n t)"),
             )
             nc.tensor.matmul_mx(
                 out=scores[c][:],
                 lhsT=q_codes[:].bitcast(FP8X4),
                 lhsT_scale=q_scales[:],
-                rhs=u_codes[c][:].bitcast(FP8X4),
-                rhs_scale=u_scales[c][:],
+                rhs=u_codes[:, cols].bitcast(FP8X4),
+                rhs_scale=u_scales[:, cols],
                 start=True,
                 stop=True,
             )
 
+        def bias(c):
+            nc.vector.tensor_tensor(neg_x[:, chunks[c]], neg_b[:, chunks[c]], scores[c][:], ALU.subtract)
+
+        def least(c, cols, before):
+            if before is None:
+                nc.vector.tensor_reduce(mins[c][:], neg_x[:, cols], AX.X, ALU.min)
+            else:
+                nc.vector.tensor_scalar(
+                    spare[:, cols], neg_x[:, cols], 1.0, mins[before][:], ALU.mult, ALU.min, accum_out=mins[c][:]
+                )
+
+        def quantise_q():
+            nc.scalar.copy(q_bf[:], q_raw[:].rearrange("p t m -> p m t"))
+            nc.vector.quantize_mx(
+                out=q_codes[:].bitcast(FP8X4), scales=q_scales[:], in_=q_bf[:].rearrange("p m t -> p (m t)")
+            )
+
+        last_gather(0)
+        last_gather(1)
+        join(0)
+        last_gather(2)
+        join(1)
+        quantise_q()
+        last_gather(3)
+        join(2)
         score(0)
-        add_pair(2, chunks[1])
-        nc.vector.tensor_tensor(neg_x[:, chunks[0]], neg_b[:, chunks[0]], scores[0][:], ALU.subtract)
+        join(3)
         score(1)
-        first_min = pool.tile([P, 1], F32, name="first_min")
-        nc.vector.tensor_reduce(first_min[:], neg_x[:, chunks[0]], AX.X, ALU.min)
-        nc.vector.tensor_tensor(neg_x[:, chunks[1]], neg_b[:, chunks[1]], scores[1][:], ALU.subtract)
-        neg_m = pool.tile([P, 1], F32, name="neg_m")
-        spare = pool.tile([P, CW], F32, name="spare")
-        nc.vector.tensor_scalar(
-            spare[:], neg_x[:, chunks[1]], 1.0, first_min[:], ALU.mult, ALU.min, accum_out=neg_m[:]
-        )
+        score(2)
+        bias(0)
+        bias(1)
+        score(3)
+        bias(2)
+        least(1, slice(0, 256), None)
+        bias(3)
+        least(3, slice(256, 512), 1)
+        neg_m = mins[len(WIDTHS) - 1]
         e = pool.tile([P, N], F32, name="e")
         total = pool.tile([P, 1], F32, name="total")
         nc.scalar.activation(e[:], neg_x[:], ACT.Exp, bias=neg_m[:], scale=-1.0, accum_out=total[:])
         inv = pool.tile([P, 1], F32, name="inv")
         nc.vector.reciprocal(inv[:], total[:])
         y = pool.tile([P, N], F32, name="y")
-        nc.vector.tensor_scalar_mul(y[:], e[:], inv[:])
-        nc.sync.dma_start(out[0], y[:])
+        for cols, queue in ((slice(0, N // 2), nc.sync), (slice(N // 2, N), nc.scalar)):
+            nc.vector.tensor_scalar_mul(y[:, cols], e[:, cols], inv[:])
+            queue.dma_start(out[0, :, cols], y[:, cols])

@@ -40,13 +40,13 @@ def tile_attend_pre_ropew_f_topk_kernel(tc, qT, kT, cT, wT, kb, offs, offs2, out
         c_rows = cT.rearrange("(p t) n -> t p n", t=PACK)
         w_rows = wT.rearrange("(p t) n -> t p n", t=PACK)
 
+        nc.scalar.dma_start(b_win[P - 1 : P, :], kb[0:1, :])
         warm = pool.tile([P, 8], F32, name="warm")
         warm_out = pool.tile([P, 8], F32, name="warm_out")
         nc.gpsimd.memset(warm[:], 0.0)
         nc.scalar.activation(warm_out[:], warm[:], ACT.Exp)
 
         nc.sync.dma_start(tok[:], offs)
-        nc.sync.dma_start(b_win[P - 1 : P, :], kb[0:1, :])
         nc.sync.dma_start(k_win[0][:], k_rows[0])
         nc.sync.dma_start(pos[:], offs2)
         nc.vector.memset(b_win[0 : P - 1, :], 0.0)
@@ -83,6 +83,29 @@ def tile_attend_pre_ropew_f_topk_kernel(tc, qT, kT, cT, wT, kb, offs, offs2, out
                 ALU.add,
             )
 
+        backs = [psum.tile([P, 2, P], F32, name="back%d" % c) for c in range(2)]
+
+        def first_pair_on_tensor():
+            turned_u = pool.tile([P, N // P, P, 2], BF16, name="turned_u", align_bytes=64)
+            for half, tag in enumerate(("turned", "spread")):
+                sums = psum.tile([P, 2, 2, P], F32, name=tag)
+                for c in range(2):
+                    cols = slice((2 * half + c) * P, (2 * half + c + 1) * P)
+                    for t in range(2):
+                        for term, first in ((kc, True), (kw, False)):
+                            nc.tensor.matmul(
+                                sums[:, c, t, :], term[:, t, cols], ident[:],
+                                start=first, stop=not first, is_transpose=True,
+                            )
+                nc.scalar.copy(turned_u[:, 2 * half : 2 * half + 2, :, :], sums[:].rearrange("s c t p -> s c p t"))
+            words = turned_u[:].rearrange("s c p t -> s (c p t)").bitcast(F32)
+            for c in range(2):
+                nc.tensor.transpose(backs[c][:, 0, :], words[:, c * P : (c + 1) * P], ident[:])
+            rest = psum.tile([P, 2 * P], F32, name="scores3")
+            for c in range(2):
+                nc.tensor.transpose(rest[:, c * P : (c + 1) * P], words[:, (2 + c) * P : (3 + c) * P], ident[:])
+            nc.scalar.copy(pair_words[:, 2 * P : N, 0], rest[:])
+
         nc.vector.tensor_copy(bg[:], b_win[:].indirect(tok[:]))
         turned = psum.tile([P, N // P, P], F32, name="turned")
         for c in range(N // P):
@@ -95,18 +118,15 @@ def tile_attend_pre_ropew_f_topk_kernel(tc, qT, kT, cT, wT, kb, offs, offs2, out
 
         for even in (0, 2):
             odd = even + 1
-            if even:
-                add_pair(0, slice(0, N // 2))
             nc.vector.tensor_copy(kg[:, even, :], k_win[even][:].indirect(tok[:]))
-            if even:
-                add_pair(0, slice(N // 2, N))
             nc.vector.tensor_tensor(kc[:, even, :], c_win[even][:].indirect(pos[:]), kg[:, even, :], ALU.mult)
             nc.vector.tensor_copy(kg[:, odd, :], k_win[odd][:].indirect(tok[:]))
             nc.scalar.activation(neg_kg[:, even // 2, :], kg[:, odd, :], ACT.Copy, scale=-1.0)
             nc.vector.tensor_tensor(kw[:, odd, :], w_win[odd][:].indirect(pos[:]), kg[:, even, :], ALU.mult)
-            nc.vector.tensor_tensor(kc[:, odd, :], c_win[odd][:].indirect(pos[:]), kg[:, odd, :], ALU.mult)
             if even == 0:
+                nc.vector.tensor_tensor(kc[:, odd, :], c_win[odd][:].indirect(pos[:]), kg[:, odd, :], ALU.mult)
                 nc.vector.tensor_tensor(kw[:, 0, :], w_win[0][:].indirect(pos[:]), neg_kg[:, 0, :], ALU.mult)
+                first_pair_on_tensor()
 
         q_bf = pool.tile([P, NQ, PACK], BF16, name="q_bf", align_bytes=64)
         q_codes = pool.tile([P, NQ], U32, name="q_codes", align_bytes=64)
@@ -126,6 +146,28 @@ def tile_attend_pre_ropew_f_topk_kernel(tc, qT, kT, cT, wT, kb, offs, offs2, out
             cols = chunks[c]
             lst = pos[:, cols.start // 16 : cols.stop // 16]
             nc.vector.tensor_tensor(kw[:, 2, cols], w_win[2][:].indirect(lst), neg_kg[:, 1, cols], ALU.mult)
+
+        def cos_gather(half):
+            cols = slice(half * N // 2, (half + 1) * N // 2)
+            lst = pos[:, cols.start // 16 : cols.stop // 16]
+            nc.vector.tensor_tensor(kc[:, 3, cols], c_win[3][:].indirect(lst), kg[:, 3, cols], ALU.mult)
+
+        late = [psum.tile([P, 2, P], F32, name=tag) for tag in ("turned", "spread")]
+        late_u = pool.tile([P, 2, P, 2], BF16, name="late_u", align_bytes=64)
+
+        def turn(c, t, term):
+            nc.tensor.matmul(
+                late[c][:, t - 2, :], term[:, t, chunks[c]], ident[:],
+                start=term is kc, stop=term is kw, is_transpose=True,
+            )
+
+        def leave(c):
+            nc.scalar.copy(late_u[:, c, :, :], late[c][:].rearrange("s t p -> s p t"))
+            words = late_u[:, c, :, :].rearrange("s p t -> s (p t)").bitcast(F32)
+            nc.tensor.transpose(backs[c][:, 1, :], words, ident[:])
+
+        def join_psum(c, copy):
+            copy(u_words[:, chunks[c], :], backs[c][:].rearrange("p h n -> p n h"))
 
         def join(c):
             add_pair(2, chunks[c])
@@ -159,31 +201,46 @@ def tile_attend_pre_ropew_f_topk_kernel(tc, qT, kT, cT, wT, kb, offs, offs2, out
                     spare[:, cols], neg_x[:, cols], 1.0, mins[before][:], ALU.mult, ALU.min, accum_out=mins[c][:]
                 )
 
-        def quantise_q():
+        def round_q():
             nc.scalar.copy(q_bf[:], q_raw[:].rearrange("p t m -> p m t"))
+
+        def quantise_q():
             nc.vector.quantize_mx(
                 out=q_codes[:].bitcast(FP8X4), scales=q_scales[:], in_=q_bf[:].rearrange("p m t -> p (m t)")
             )
 
+        cos_gather(0)
+        cos_gather(1)
+        turn(0, 3, kc)
+        turn(0, 3, kw)
+        turn(1, 3, kc)
+        turn(1, 3, kw)
+        turn(0, 2, kc)
+        turn(1, 2, kc)
         last_gather(0)
+        turn(0, 2, kw)
         last_gather(1)
-        join(0)
+        turn(1, 2, kw)
+        round_q()
+        leave(0)
+        leave(1)
         last_gather(2)
-        join(1)
-        quantise_q()
         last_gather(3)
         join(2)
-        score(0)
         join(3)
-        score(1)
+        quantise_q()
+        join_psum(0, nc.vector.tensor_copy)
         score(2)
-        bias(0)
-        bias(1)
+        join_psum(1, nc.scalar.copy)
+        score(0)
         score(3)
+        score(1)
         bias(2)
-        least(1, slice(0, 256), None)
+        bias(0)
         bias(3)
-        least(3, slice(256, 512), 1)
+        least(0, slice(256, 512), None)
+        bias(1)
+        least(3, slice(0, 256), 0)
         neg_m = mins[len(WIDTHS) - 1]
         e = pool.tile([P, N], F32, name="e")
         total = pool.tile([P, 1], F32, name="total")

@@ -5,7 +5,7 @@ from concourse.masks import make_identity
 
 N, T, T2, D, NQ = 512, 2048, 1024, 512, 128
 FLOPS = 2 * NQ * N * D
-BYTES = 4 * (D * NQ + D * T + 2 * D * T2 + T + NQ * N) + 2 * 2 * 128 * (N // 16)
+BYTES = 4 * (D * NQ + D * T + D * T2 + T + NQ * N) + 2 * 2 * 128 * (N // 16)
 
 F32 = mybir.dt.float32
 BF16 = mybir.dt.bfloat16
@@ -31,8 +31,8 @@ def tile_attend_pre_ropew_f_topk_kernel(tc, qT, kT, cT, wT, kb, offs, offs2, out
         tok = pool.tile([P, N // 16], U16, name="tok")
         pos = pool.tile([P, N // 16], U16, name="pos")
         k_win = [pool.tile([P, T], F32, name="k_win%d" % t) for t in range(PACK)]
-        c_win = [pool.tile([P, T2], F32, name="c_win%d" % t) for t in range(PACK)]
-        w_win = [pool.tile([P, T2], F32, name="w_win%d" % t) for t in range(PACK)]
+        c_win = [pool.tile([P, T2], F32, name="c_win%d" % h) for h in range(2)]
+        w_win = [pool.tile([P, T2], F32, name="w_win%d" % h) for h in range(2)]
         b_win = pool.tile([P, T], F32, name="b_win")
         q_raw = pool.tile([P, PACK, NQ], F32, name="q_raw")
 
@@ -40,33 +40,24 @@ def tile_attend_pre_ropew_f_topk_kernel(tc, qT, kT, cT, wT, kb, offs, offs2, out
         c_rows = cT.rearrange("(p t) n -> t p n", t=PACK)
         w_rows = wT.rearrange("(p t) n -> t p n", t=PACK)
 
-        nc.scalar.dma_start(b_win[P - 1 : P, :], kb[0:1, :])
-        warm = pool.tile([P, 8], F32, name="warm")
-        warm_out = pool.tile([P, 8], F32, name="warm_out")
-        nc.gpsimd.memset(warm[:], 0.0)
-        nc.scalar.activation(warm_out[:], warm[:], ACT.Exp)
-
         nc.sync.dma_start(tok[:], offs)
-        nc.sync.dma_start(k_win[0][:], k_rows[0])
+        nc.sync.dma_start(b_win[P - 1 : P, :], kb[0:1, :])
+        nc.sync.dma_start(c_win[0][:], c_rows[0])
         nc.sync.dma_start(pos[:], offs2)
-        nc.vector.memset(b_win[0 : P - 1, :], 0.0)
+        nc.vector.memset(b_win[0 : P - 1, 0 : T // 2], 0.0)
+        nc.gpsimd.memset(b_win[0 : P - 1, T // 2 : T], 0.0)
         ident = pool.tile([P, P], F32, name="ident")
         make_identity(nc, ident[:])
-        for even in (0, 2):
-            odd = even + 1
-            if even:
-                nc.sync.dma_start(k_win[even][:], k_rows[even])
-            nc.sync.dma_start(c_win[even][:], c_rows[even])
-            nc.sync.dma_start(k_win[odd][:], k_rows[odd])
-            nc.sync.dma_start(w_win[odd][:], w_rows[odd])
-            nc.sync.dma_start(c_win[odd][:], c_rows[odd])
-            nc.sync.dma_start(w_win[even][:], w_rows[even])
+        nc.sync.dma_start(w_win[0][:], w_rows[0])
+        nc.sync.dma_start(c_win[1][:], c_rows[2])
+        nc.sync.dma_start(w_win[1][:], w_rows[2])
+        for t in range(PACK):
+            nc.sync.dma_start(k_win[t][:], k_rows[t])
         nc.sync.dma_start(q_raw[:], qT[0].rearrange("(p t) m -> p t m", t=PACK))
 
-        kg = pool.tile([P, PACK, N], F32, name="kg")
-        neg_kg = pool.tile([P, 2, N], F32, name="neg_kg")
-        kc = pool.tile([P, PACK, N], F32, name="kc")
-        kw = pool.tile([P, PACK, N], F32, name="kw")
+        tab = [pool.tile([P, 3, N], F32, name="tab%d" % h) for h in range(2)]
+        from_even = pool.tile([P, PACK, N], F32, name="from_even")
+        from_odd = pool.tile([P, PACK, N], F32, name="from_odd")
         u_pair = pool.tile([P, 2, N, 2], BF16, name="u_pair", align_bytes=64)
         u_bf = pool.tile([P, N, PACK], BF16, name="u_bf", align_bytes=64)
         bg = pool.tile([P, N], F32, name="bg")
@@ -78,8 +69,8 @@ def tile_attend_pre_ropew_f_topk_kernel(tc, qT, kT, cT, wT, kb, offs, offs2, out
         def add_pair(even, cols):
             nc.vector.tensor_tensor(
                 u_pair[:, even // 2, cols, :],
-                kc[:, even : even + 2, cols].rearrange("p t n -> p n t"),
-                kw[:, even : even + 2, cols].rearrange("p t n -> p n t"),
+                from_even[:, even : even + 2, cols].rearrange("p t n -> p n t"),
+                from_odd[:, even : even + 2, cols].rearrange("p t n -> p n t"),
                 ALU.add,
             )
 
@@ -92,7 +83,7 @@ def tile_attend_pre_ropew_f_topk_kernel(tc, qT, kT, cT, wT, kb, offs, offs2, out
                 for c in range(2):
                     cols = slice((2 * half + c) * P, (2 * half + c + 1) * P)
                     for t in range(2):
-                        for term, first in ((kc, True), (kw, False)):
+                        for term, first in ((from_even, True), (from_odd, False)):
                             nc.tensor.matmul(
                                 sums[:, c, t, :], term[:, t, cols], ident[:],
                                 start=first, stop=not first, is_transpose=True,
@@ -116,16 +107,25 @@ def tile_attend_pre_ropew_f_topk_kernel(tc, qT, kT, cT, wT, kb, offs, offs2, out
             nc.tensor.transpose(spread[:, c * P : (c + 1) * P], b_col[:, c : c + 1].to_broadcast([P, P]), ident[:])
         nc.scalar.copy(neg_b[:], spread[:])
 
-        for even in (0, 2):
-            odd = even + 1
-            nc.vector.tensor_copy(kg[:, even, :], k_win[even][:].indirect(tok[:]))
-            nc.vector.tensor_tensor(kc[:, even, :], c_win[even][:].indirect(pos[:]), kg[:, even, :], ALU.mult)
-            nc.vector.tensor_copy(kg[:, odd, :], k_win[odd][:].indirect(tok[:]))
-            nc.scalar.activation(neg_kg[:, even // 2, :], kg[:, odd, :], ACT.Copy, scale=-1.0)
-            nc.vector.tensor_tensor(kw[:, odd, :], w_win[odd][:].indirect(pos[:]), kg[:, even, :], ALU.mult)
-            if even == 0:
-                nc.vector.tensor_tensor(kc[:, odd, :], c_win[odd][:].indirect(pos[:]), kg[:, odd, :], ALU.mult)
-                nc.vector.tensor_tensor(kw[:, 0, :], w_win[0][:].indirect(pos[:]), neg_kg[:, 0, :], ALU.mult)
+        for h in range(2):
+            nc.vector.tensor_copy(tab[h][:, 1, :], c_win[h][:].indirect(pos[:]))
+            nc.vector.tensor_copy(tab[h][:, 2, :], w_win[h][:].indirect(pos[:]))
+            nc.scalar.activation(tab[h][:, 0, :], tab[h][:, 2, :], ACT.Copy, scale=-1.0)
+
+        def rotate(t, j, cols):
+            h, odd = divmod(t, 2)
+            lst = tok[:, cols.start // 16 : cols.stop // 16]
+            nc.vector.tensor_tensor(
+                (from_odd if odd else from_even)[:, 2 * h + j, cols],
+                k_win[t][:].indirect(lst),
+                tab[h][:, 1 - odd + j, cols],
+                ALU.mult,
+            )
+
+        for t in range(PACK - 1):
+            for j in range(2):
+                rotate(t, j, slice(0, N))
+            if t == 1:
                 first_pair_on_tensor()
 
         q_bf = pool.tile([P, NQ, PACK], BF16, name="q_bf", align_bytes=64)
@@ -142,23 +142,13 @@ def tile_attend_pre_ropew_f_topk_kernel(tc, qT, kT, cT, wT, kb, offs, offs2, out
         mins = [pool.tile([P, 1], F32, name="min%d" % c) for c in range(len(WIDTHS))]
         spare = pool.tile([P, N], F32, name="spare")
 
-        def last_gather(c):
-            cols = chunks[c]
-            lst = pos[:, cols.start // 16 : cols.stop // 16]
-            nc.vector.tensor_tensor(kw[:, 2, cols], w_win[2][:].indirect(lst), neg_kg[:, 1, cols], ALU.mult)
-
-        def cos_gather(half):
-            cols = slice(half * N // 2, (half + 1) * N // 2)
-            lst = pos[:, cols.start // 16 : cols.stop // 16]
-            nc.vector.tensor_tensor(kc[:, 3, cols], c_win[3][:].indirect(lst), kg[:, 3, cols], ALU.mult)
-
         late = [psum.tile([P, 2, P], F32, name=tag) for tag in ("turned", "spread")]
         late_u = pool.tile([P, 2, P, 2], BF16, name="late_u", align_bytes=64)
 
         def turn(c, t, term):
             nc.tensor.matmul(
                 late[c][:, t - 2, :], term[:, t, chunks[c]], ident[:],
-                start=term is kc, stop=term is kw, is_transpose=True,
+                start=term is from_even, stop=term is from_odd, is_transpose=True,
             )
 
         def leave(c):
@@ -209,23 +199,17 @@ def tile_attend_pre_ropew_f_topk_kernel(tc, qT, kT, cT, wT, kb, offs, offs2, out
                 out=q_codes[:].bitcast(FP8X4), scales=q_scales[:], in_=q_bf[:].rearrange("p m t -> p (m t)")
             )
 
-        cos_gather(0)
-        cos_gather(1)
-        turn(0, 3, kc)
-        turn(0, 3, kw)
-        turn(1, 3, kc)
-        turn(1, 3, kw)
-        turn(0, 2, kc)
-        turn(1, 2, kc)
-        last_gather(0)
-        turn(0, 2, kw)
-        last_gather(1)
-        turn(1, 2, kw)
+        for c in range(2):
+            for t in (2, 3):
+                rotate(3, t - 2, chunks[c])
+                turn(c, t, from_even)
+                turn(c, t, from_odd)
         round_q()
         leave(0)
         leave(1)
-        last_gather(2)
-        last_gather(3)
+        for c in (2, 3):
+            for j in range(2):
+                rotate(3, j, chunks[c])
         join(2)
         join(3)
         quantise_q()

@@ -19,7 +19,7 @@ AX = mybir.AxisListType
 
 P = 128
 PACK = 4
-WIDTHS = (128, 128, 128, 128)
+ON_TENSOR = 2
 
 
 def tile_attend_pre_ropew_f_topk_kernel(tc, qT, kT, cT, wT, kb, offs, offs2, out):
@@ -49,65 +49,41 @@ def tile_attend_pre_ropew_f_topk_kernel(tc, qT, kT, cT, wT, kb, offs, offs2, out
         ident = pool.tile([P, P], F32, name="ident")
         make_identity(nc, ident[:])
         nc.sync.dma_start(w_win[0][:], w_rows[0])
-        nc.sync.dma_start(c_win[1][:], c_rows[2])
-        nc.sync.dma_start(w_win[1][:], w_rows[2])
-        for t in range(PACK):
+        for t in range(2):
             nc.sync.dma_start(k_win[t][:], k_rows[t])
+        nc.sync.dma_start(c_win[1][:], c_rows[2])
+        nc.sync.dma_start(k_win[3][:], k_rows[3])
+        nc.sync.dma_start(w_win[1][:], w_rows[2])
+        nc.sync.dma_start(k_win[2][:], k_rows[2])
         nc.sync.dma_start(q_raw[:], qT[0].rearrange("(p t) m -> p t m", t=PACK))
 
+        chunks = [slice(c * P, (c + 1) * P) for c in range(N // P)]
         tab = [pool.tile([P, 3, N], F32, name="tab%d" % h) for h in range(2)]
         from_even = pool.tile([P, PACK, N], F32, name="from_even")
         from_odd = pool.tile([P, PACK, N], F32, name="from_odd")
-        u_pair = pool.tile([P, 2, N, 2], BF16, name="u_pair", align_bytes=64)
-        u_bf = pool.tile([P, N, PACK], BF16, name="u_bf", align_bytes=64)
+        runs = [slice(0, 2 * P), chunks[2], chunks[3]]
+        u_pair = [pool.tile([P, 2, P, 2], BF16, name="u_pair%d" % c, align_bytes=64) for c in range(1)]
+        pair_words = [u[:].rearrange("p h n e -> p (h n e)").bitcast(F32).rearrange("p (h n) -> p h n", h=2) for u in u_pair]
+        u_bf = {}
+
+        def words_of(i):
+            return u_bf[i][:].rearrange("p n t -> p (n t)").bitcast(F32).rearrange("p (n h) -> p n h", h=2)
+
         bg = pool.tile([P, N], F32, name="bg")
         b_col = pool.tile([P, N // P], F32, name="b_col")
         neg_b = pool.tile([P, N], F32, name="neg_b")
-        pair_words = u_pair[:].rearrange("p h n e -> p (h n e)").bitcast(F32).rearrange("p (h n) -> p n h", h=2)
-        u_words = u_bf[:].rearrange("p n t -> p (n t)").bitcast(F32).rearrange("p (n h) -> p n h", h=2)
-
-        def add_pair(even, cols):
-            nc.vector.tensor_tensor(
-                u_pair[:, even // 2, cols, :],
-                from_even[:, even : even + 2, cols].rearrange("p t n -> p n t"),
-                from_odd[:, even : even + 2, cols].rearrange("p t n -> p n t"),
-                ALU.add,
-            )
-
-        backs = [psum.tile([P, 2, P], F32, name="back%d" % c) for c in range(2)]
-
-        def first_pair_on_tensor():
-            turned_u = pool.tile([P, N // P, P, 2], BF16, name="turned_u", align_bytes=64)
-            for half, tag in enumerate(("turned", "spread")):
-                sums = psum.tile([P, 2, 2, P], F32, name=tag)
-                for c in range(2):
-                    cols = slice((2 * half + c) * P, (2 * half + c + 1) * P)
-                    for t in range(2):
-                        for term, first in ((from_even, True), (from_odd, False)):
-                            nc.tensor.matmul(
-                                sums[:, c, t, :], term[:, t, cols], ident[:],
-                                start=first, stop=not first, is_transpose=True,
-                            )
-                nc.scalar.copy(turned_u[:, 2 * half : 2 * half + 2, :, :], sums[:].rearrange("s c t p -> s c p t"))
-            words = turned_u[:].rearrange("s c p t -> s (c p t)").bitcast(F32)
-            for c in range(2):
-                nc.tensor.transpose(backs[c][:, 0, :], words[:, c * P : (c + 1) * P], ident[:])
-            rest = psum.tile([P, 2 * P], F32, name="scores3")
-            for c in range(2):
-                nc.tensor.transpose(rest[:, c * P : (c + 1) * P], words[:, (2 + c) * P : (3 + c) * P], ident[:])
-            nc.scalar.copy(pair_words[:, 2 * P : N, 0], rest[:])
 
         nc.vector.tensor_copy(bg[:], b_win[:].indirect(tok[:]))
         turned = psum.tile([P, N // P, P], F32, name="turned")
         for c in range(N // P):
-            nc.tensor.transpose(turned[:, c, :], bg[:, c * P : (c + 1) * P], ident[:])
+            nc.tensor.transpose(turned[:, c, :], bg[:, chunks[c]], ident[:])
         nc.scalar.activation(b_col[:], turned[:, :, P - 1], ACT.Copy, scale=-1.0)
         spread = psum.tile([P, N], F32, name="spread")
         for c in range(N // P):
-            nc.tensor.transpose(spread[:, c * P : (c + 1) * P], b_col[:, c : c + 1].to_broadcast([P, P]), ident[:])
+            nc.tensor.transpose(spread[:, chunks[c]], b_col[:, c : c + 1].to_broadcast([P, P]), ident[:])
         nc.scalar.copy(neg_b[:], spread[:])
 
-        for h in range(2):
+        for h in range(1):
             nc.vector.tensor_copy(tab[h][:, 1, :], c_win[h][:].indirect(pos[:]))
             nc.vector.tensor_copy(tab[h][:, 2, :], w_win[h][:].indirect(pos[:]))
             nc.scalar.activation(tab[h][:, 0, :], tab[h][:, 2, :], ACT.Copy, scale=-1.0)
@@ -122,66 +98,98 @@ def tile_attend_pre_ropew_f_topk_kernel(tc, qT, kT, cT, wT, kb, offs, offs2, out
                 ALU.mult,
             )
 
-        for t in range(PACK - 1):
+        def turn(bank, term, t, c, start, stop):
+            nc.tensor.matmul(bank, term[:, t, chunks[c]], ident[:], start=start, stop=stop, is_transpose=True)
+
+        backs = [psum.tile([P, 2, P], F32, name="back%d" % c) for c in range(ON_TENSOR)]
+        early = [psum.tile([P, 2, 2, P], F32, name=tag) for tag in ("turned", "spread")]
+        kg = pool.tile([P, 3, N], F32, name="kg")
+        for t in range(2):
+            if t:
+                nc.vector.tensor_copy(kg[:, t, :], k_win[t][:].indirect(tok[:]))
             for j in range(2):
-                rotate(t, j, slice(0, N))
-            if t == 1:
-                first_pair_on_tensor()
+                if t:
+                    nc.gpsimd.tensor_tensor(from_odd[:, j, :], tab[0][:, j, :], kg[:, t, :], ALU.mult)
+                else:
+                    rotate(t, j, slice(0, N))
+                for c in range(N // P):
+                    turn(
+                        early[c // 2][:, c % 2, j, :], (from_even, from_odd)[t], j, c,
+                        (t, j, c % 2) == (0, 0, 0), (t, j, c % 2) == (1, 1, 1),
+                    )
+        turned_u = pool.tile([P, N // P, P, 2], BF16, name="turned_u", align_bytes=64)
+        for half in range(2):
+            nc.scalar.copy(turned_u[:, 2 * half : 2 * half + 2, :, :], early[half][:].rearrange("s c t p -> s c p t"))
+        words = turned_u[:].rearrange("s c p t -> s (c p t)").bitcast(F32)
+        for c in range(ON_TENSOR):
+            nc.tensor.transpose(backs[c][:, 0, :], words[:, chunks[c]], ident[:])
+        rest = psum.tile([P, 2, P], F32, name="rest")
+        for c in range(2):
+            nc.tensor.transpose(rest[:, c, :], words[:, chunks[2 + c]], ident[:])
+        u_bf[2] = pool.tile([P, P, PACK], BF16, name="u_bf2", align_bytes=64)
+        nc.scalar.copy(pair_words[0][:, 0, :], rest[:, 0, :])
+        nc.scalar.copy(words_of(2)[:, :, 0], rest[:, 1, :])
+
+        late_tags = ("turned", "spread")
+        late = [psum.tile([P, 2, P], F32, name=tag) for tag in late_tags]
+        late_u = [pool.tile([P, P, 2], BF16, name="late_u%d" % c, align_bytes=64) for c in range(ON_TENSOR)]
+        nc.vector.tensor_copy(tab[1][:, 1, :], c_win[1][:].indirect(pos[:]))
+        nc.vector.tensor_copy(kg[:, 2, :], k_win[3][:].indirect(tok[:]))
+        nc.gpsimd.tensor_tensor(from_odd[:, 3, :], tab[1][:, 1, :], kg[:, 2, :], ALU.mult)
+        nc.vector.tensor_copy(tab[1][:, 2, :], w_win[1][:].indirect(pos[:]))
+        nc.vector.scalar_tensor_tensor(from_odd[:, 2, :], kg[:, 2, :], -1.0, tab[1][:, 2, :], ALU.mult, ALU.mult)
+        for j in (1, 0):
+            for c in range(ON_TENSOR):
+                turn(late[c][:, j, :], from_odd, 2 + j, c, j == 1, False)
 
         q_bf = pool.tile([P, NQ, PACK], BF16, name="q_bf", align_bytes=64)
         q_codes = pool.tile([P, NQ], U32, name="q_codes", align_bytes=64)
         q_scales = pool.tile([P, NQ], U8, name="q_scales", align_bytes=64)
-        u_codes = pool.tile([P, N], U32, name="u_codes", align_bytes=64)
         u_scales = pool.tile([P, N], U8, name="u_scales", align_bytes=64)
-        chunks = []
-        for w in WIDTHS:
-            first = chunks[-1].stop if chunks else 0
-            chunks.append(slice(first, first + w))
-        scores = [psum.tile([P, w], F32, name="scores%d" % c) for c, w in enumerate(WIDTHS)]
-        neg_x = pool.tile([P, N], F32, name="neg_x")
-        mins = [pool.tile([P, 1], F32, name="min%d" % c) for c in range(len(WIDTHS))]
+        scores = {}
+        mins = [pool.tile([P, 1], F32, name="min%d" % c) for c in range(N // P)]
         spare = pool.tile([P, N], F32, name="spare")
 
-        late = [psum.tile([P, 2, P], F32, name=tag) for tag in ("turned", "spread")]
-        late_u = pool.tile([P, 2, P, 2], BF16, name="late_u", align_bytes=64)
-
-        def turn(c, t, term):
-            nc.tensor.matmul(
-                late[c][:, t - 2, :], term[:, t, chunks[c]], ident[:],
-                start=term is from_even, stop=term is from_odd, is_transpose=True,
-            )
-
         def leave(c):
-            nc.scalar.copy(late_u[:, c, :, :], late[c][:].rearrange("s t p -> s p t"))
-            words = late_u[:, c, :, :].rearrange("s p t -> s (p t)").bitcast(F32)
-            nc.tensor.transpose(backs[c][:, 1, :], words, ident[:])
-
-        def join_psum(c, copy):
-            copy(u_words[:, chunks[c], :], backs[c][:].rearrange("p h n -> p n h"))
+            nc.scalar.copy(late_u[c][:], late[c][:].rearrange("s t p -> s p t"))
+            nc.tensor.transpose(backs[c][:, 1, :], late_u[c][:].rearrange("s p t -> s (p t)").bitcast(F32), ident[:])
 
         def join(c):
-            add_pair(2, chunks[c])
-            nc.scalar.copy(u_words[:, chunks[c], :], pair_words[:, chunks[c], :])
+            nc.scalar.copy(words_of(0)[:, chunks[c], :], backs[c][:].rearrange("p h n -> p n h"))
 
-        def score(c):
-            cols = chunks[c]
-            nc.vector.quantize_mx(
-                out=u_codes[:, cols].bitcast(FP8X4),
-                scales=u_scales[:, cols],
-                in_=u_bf[:, cols, :].rearrange("p n t -> p (n t)"),
+        def add_pair(c):
+            nc.vector.tensor_tensor(
+                u_pair[0][:, 1, :, :] if c == 2 else u_bf[2][:, :, 2:PACK],
+                from_even[:, 2:PACK, chunks[c]].rearrange("p t n -> p n t"),
+                from_odd[:, 2:PACK, chunks[c]].rearrange("p t n -> p n t"),
+                ALU.add,
             )
+            if c == 2:
+                u_bf[1] = pool.tile([P, P, PACK], BF16, name="late_u1", align_bytes=64)
+                nc.scalar.copy(words_of(1), pair_words[0].rearrange("p h n -> p n h"))
+
+        def score(i):
+            cols = runs[i]
+            width = cols.stop - cols.start
+            codes = pool.tile([P, width], U32, name="codes%d" % i, align_bytes=64)
+            nc.vector.quantize_mx(
+                out=codes[:].bitcast(FP8X4),
+                scales=u_scales[:, cols],
+                in_=u_bf[i][:].rearrange("p n t -> p (n t)"),
+            )
+            scores[i] = psum.tile([P, width], F32, name="scores%d" % i)
             nc.tensor.matmul_mx(
-                out=scores[c][:],
+                out=scores[i][:],
                 lhsT=q_codes[:].bitcast(FP8X4),
                 lhsT_scale=q_scales[:],
-                rhs=u_codes[:, cols].bitcast(FP8X4),
+                rhs=codes[:].bitcast(FP8X4),
                 rhs_scale=u_scales[:, cols],
                 start=True,
                 stop=True,
             )
 
-        def bias(c):
-            nc.vector.tensor_tensor(neg_x[:, chunks[c]], neg_b[:, chunks[c]], scores[c][:], ALU.subtract)
+        def bias(i):
+            nc.vector.tensor_tensor(neg_x[:, runs[i]], neg_b[:, runs[i]], scores[i][:], ALU.subtract)
 
         def least(c, cols, before):
             if before is None:
@@ -191,41 +199,30 @@ def tile_attend_pre_ropew_f_topk_kernel(tc, qT, kT, cT, wT, kb, offs, offs2, out
                     spare[:, cols], neg_x[:, cols], 1.0, mins[before][:], ALU.mult, ALU.min, accum_out=mins[c][:]
                 )
 
-        def round_q():
-            nc.scalar.copy(q_bf[:], q_raw[:].rearrange("p t m -> p m t"))
-
-        def quantise_q():
-            nc.vector.quantize_mx(
-                out=q_codes[:].bitcast(FP8X4), scales=q_scales[:], in_=q_bf[:].rearrange("p m t -> p (m t)")
-            )
-
-        for c in range(2):
-            for t in (2, 3):
-                rotate(3, t - 2, chunks[c])
-                turn(c, t, from_even)
-                turn(c, t, from_odd)
-        round_q()
-        leave(0)
-        leave(1)
-        for c in (2, 3):
+        for c in range(N // P):
             for j in range(2):
-                rotate(3, j, chunks[c])
-        join(2)
-        join(3)
-        quantise_q()
-        join_psum(0, nc.vector.tensor_copy)
-        score(2)
-        join_psum(1, nc.scalar.copy)
-        score(0)
-        score(3)
-        score(1)
-        bias(2)
-        bias(0)
-        bias(3)
-        least(0, slice(256, 512), None)
-        bias(1)
-        least(3, slice(0, 256), 0)
-        neg_m = mins[len(WIDTHS) - 1]
+                rotate(2, j, chunks[c])
+                if c < ON_TENSOR:
+                    turn(late[c][:, j, :], from_even, 2 + j, c, False, j == 1)
+            if c == 0:
+                nc.scalar.copy(q_bf[:], q_raw[:].rearrange("p t m -> p m t"))
+            if c < ON_TENSOR:
+                leave(c)
+        u_bf[0] = pool.tile([P, 2 * P, PACK], BF16, name="u_bf0", align_bytes=64)
+        join(0)
+        join(1)
+        add_pair(2)
+        add_pair(3)
+        nc.vector.quantize_mx(
+            out=q_codes[:].bitcast(FP8X4), scales=q_scales[:], in_=q_bf[:].rearrange("p m t -> p (m t)")
+        )
+        for i in (2, 0, 1):
+            score(i)
+        neg_x = pool.tile([P, N], F32, name="late_u1", align_bytes=64)
+        for i in (2, 0, 1):
+            bias(i)
+        least(3, slice(0, N), None)
+        neg_m = mins[3]
         e = pool.tile([P, N], F32, name="e")
         total = pool.tile([P, 1], F32, name="total")
         nc.scalar.activation(e[:], neg_x[:], ACT.Exp, bias=neg_m[:], scale=-1.0, accum_out=total[:])

@@ -19,6 +19,7 @@ AX = mybir.AxisListType
 
 P = 128
 PACK = 4
+CHUNKS = N // P
 ON_TENSOR = 2
 
 
@@ -27,6 +28,12 @@ def tile_attend_pre_ropew_f_topk_kernel(tc, qT, kT, cT, wT, kb, offs, offs2, out
     with ExitStack() as ctx:
         pool = ctx.enter_context(tc.tile_pool(name="held", bufs=1))
         psum = ctx.enter_context(tc.psum_pool(name="psum", bufs=1))
+
+        def list_columns(cols):
+            return slice(cols.start // 16, cols.stop // 16)
+
+        def as_word_pairs(interleaved):
+            return interleaved[:].rearrange("p n t -> p (n t)").bitcast(F32).rearrange("p (n h) -> p n h", h=2)
 
         tok = pool.tile([P, N // 16], U16, name="tok")
         pos = pool.tile([P, N // 16], U16, name="pos")
@@ -40,12 +47,11 @@ def tile_attend_pre_ropew_f_topk_kernel(tc, qT, kT, cT, wT, kb, offs, offs2, out
         c_rows = cT.rearrange("(p t) n -> t p n", t=PACK)
         w_rows = wT.rearrange("(p t) n -> t p n", t=PACK)
 
-        nc.sync.dma_start(tok[:], offs)
-        nc.sync.dma_start(b_win[P - 1 : P, :], kb[0:1, :])
         nc.sync.dma_start(c_win[0][:], c_rows[0])
         nc.sync.dma_start(pos[:], offs2)
-        nc.vector.memset(b_win[0 : P - 1, 0 : T // 2], 0.0)
-        nc.gpsimd.memset(b_win[0 : P - 1, T // 2 : T], 0.0)
+        nc.sync.dma_start(tok[:], offs)
+        nc.sync.dma_start(b_win[P - 1 : P, :], kb[0:1, :])
+        nc.vector.memset(b_win[0 : P - 1, :], 0.0)
         ident = pool.tile([P, P], F32, name="ident")
         make_identity(nc, ident[:])
         nc.sync.dma_start(w_win[0][:], w_rows[0])
@@ -57,129 +63,123 @@ def tile_attend_pre_ropew_f_topk_kernel(tc, qT, kT, cT, wT, kb, offs, offs2, out
         nc.sync.dma_start(k_win[2][:], k_rows[2])
         nc.sync.dma_start(q_raw[:], qT[0].rearrange("(p t) m -> p t m", t=PACK))
 
-        chunks = [slice(c * P, (c + 1) * P) for c in range(N // P)]
-        tab = [pool.tile([P, 3, N], F32, name="tab%d" % h) for h in range(2)]
+        chunks = [slice(c * P, (c + 1) * P) for c in range(CHUNKS)]
         from_even = pool.tile([P, PACK, N], F32, name="from_even")
         from_odd = pool.tile([P, PACK, N], F32, name="from_odd")
-        runs = [slice(0, 2 * P), chunks[2], chunks[3]]
-        u_pair = [pool.tile([P, 2, P, 2], BF16, name="u_pair%d" % c, align_bytes=64) for c in range(1)]
-        pair_words = [u[:].rearrange("p h n e -> p (h n e)").bitcast(F32).rearrange("p (h n) -> p h n", h=2) for u in u_pair]
-        u_bf = {}
 
-        def words_of(i):
-            return u_bf[i][:].rearrange("p n t -> p (n t)").bitcast(F32).rearrange("p (n h) -> p n h", h=2)
+        first_tables = pool.tile([P, 3, N], F32, name="first_tables")
+        nc.vector.tensor_copy(first_tables[:, 1, :], c_win[0][:].indirect(pos[:]))
+        nc.vector.tensor_copy(first_tables[:, 2, :], w_win[0][:].indirect(pos[:]))
+        nc.scalar.activation(first_tables[:, 0, :], first_tables[:, 2, :], ACT.Copy, scale=-1.0)
 
-        bg = pool.tile([P, N], F32, name="bg")
-        b_col = pool.tile([P, N // P], F32, name="b_col")
+        b_row = pool.tile([P, N], F32, name="b_row")
+        b_col = pool.tile([P, CHUNKS], F32, name="b_col")
         neg_b = pool.tile([P, N], F32, name="neg_b")
+        nc.vector.tensor_copy(b_row[:], b_win[:].indirect(tok[:]))
+        b_turned = psum.tile([P, CHUNKS, P], F32, name="bank0")
+        for c in range(CHUNKS):
+            nc.tensor.transpose(b_turned[:, c, :], b_row[:, chunks[c]], ident[:])
+        nc.scalar.activation(b_col[:], b_turned[:, :, P - 1], ACT.Copy, scale=-1.0)
+        b_spread = psum.tile([P, N], F32, name="bank1")
+        for c in range(CHUNKS):
+            nc.tensor.transpose(b_spread[:, chunks[c]], b_col[:, c : c + 1].to_broadcast([P, P]), ident[:])
+        nc.scalar.copy(neg_b[:], b_spread[:])
 
-        nc.vector.tensor_copy(bg[:], b_win[:].indirect(tok[:]))
-        turned = psum.tile([P, N // P, P], F32, name="turned")
-        for c in range(N // P):
-            nc.tensor.transpose(turned[:, c, :], bg[:, chunks[c]], ident[:])
-        nc.scalar.activation(b_col[:], turned[:, :, P - 1], ACT.Copy, scale=-1.0)
-        spread = psum.tile([P, N], F32, name="spread")
-        for c in range(N // P):
-            nc.tensor.transpose(spread[:, chunks[c]], b_col[:, c : c + 1].to_broadcast([P, P]), ident[:])
-        nc.scalar.copy(neg_b[:], spread[:])
+        def turn_and_add(target, term, start, stop):
+            nc.tensor.matmul(target, term, ident[:], start=start, stop=stop, is_transpose=True)
 
-        for h in range(1):
-            nc.vector.tensor_copy(tab[h][:, 1, :], c_win[h][:].indirect(pos[:]))
-            nc.vector.tensor_copy(tab[h][:, 2, :], w_win[h][:].indirect(pos[:]))
-            nc.scalar.activation(tab[h][:, 0, :], tab[h][:, 2, :], ACT.Copy, scale=-1.0)
-
-        def rotate(t, j, cols):
-            h, odd = divmod(t, 2)
-            lst = tok[:, cols.start // 16 : cols.stop // 16]
-            nc.vector.tensor_tensor(
-                (from_odd if odd else from_even)[:, 2 * h + j, cols],
-                k_win[t][:].indirect(lst),
-                tab[h][:, 1 - odd + j, cols],
-                ALU.mult,
-            )
-
-        def turn(bank, term, t, c, start, stop):
-            nc.tensor.matmul(bank, term[:, t, chunks[c]], ident[:], start=start, stop=stop, is_transpose=True)
-
-        backs = [psum.tile([P, 2, P], F32, name="back%d" % c) for c in range(ON_TENSOR)]
-        early = [psum.tile([P, 2, 2, P], F32, name=tag) for tag in ("turned", "spread")]
-        kg = pool.tile([P, 3, N], F32, name="kg")
+        word_banks = [psum.tile([P, 2, P], F32, name="words%d" % c) for c in range(ON_TENSOR)]
+        first_sums = [psum.tile([P, 2, 2, P], F32, name="bank%d" % half) for half in range(2)]
+        keys = pool.tile([P, 3, N], F32, name="keys")
         for t in range(2):
-            if t:
-                nc.vector.tensor_copy(kg[:, t, :], k_win[t][:].indirect(tok[:]))
+            term = (from_even, from_odd)[t]
+            nc.vector.tensor_copy(keys[:, t, :], k_win[t][:].indirect(tok[:]))
             for j in range(2):
-                if t:
-                    nc.gpsimd.tensor_tensor(from_odd[:, j, :], tab[0][:, j, :], kg[:, t, :], ALU.mult)
-                else:
-                    rotate(t, j, slice(0, N))
-                for c in range(N // P):
-                    turn(
-                        early[c // 2][:, c % 2, j, :], (from_even, from_odd)[t], j, c,
-                        (t, j, c % 2) == (0, 0, 0), (t, j, c % 2) == (1, 1, 1),
+                nc.gpsimd.tensor_tensor(term[:, j, :], first_tables[:, 1 - t + j, :], keys[:, t, :], ALU.mult)
+                for c in range(CHUNKS):
+                    half, inner = divmod(c, 2)
+                    turn_and_add(
+                        first_sums[half][:, inner, j, :], term[:, j, chunks[c]],
+                        start=(t, j, inner) == (0, 0, 0), stop=(t, j, inner) == (1, 1, 1),
                     )
-        turned_u = pool.tile([P, N // P, P, 2], BF16, name="turned_u", align_bytes=64)
+        first_u = pool.tile([P, CHUNKS, P, 2], BF16, name="first_u", align_bytes=64)
         for half in range(2):
-            nc.scalar.copy(turned_u[:, 2 * half : 2 * half + 2, :, :], early[half][:].rearrange("s c t p -> s c p t"))
-        words = turned_u[:].rearrange("s c p t -> s (c p t)").bitcast(F32)
+            nc.scalar.copy(first_u[:, 2 * half : 2 * half + 2, :, :], first_sums[half][:].rearrange("s c t p -> s c p t"))
+        first_words = first_u[:].rearrange("s c p t -> s (c p t)").bitcast(F32)
         for c in range(ON_TENSOR):
-            nc.tensor.transpose(backs[c][:, 0, :], words[:, chunks[c]], ident[:])
-        rest = psum.tile([P, 2, P], F32, name="rest")
-        for c in range(2):
-            nc.tensor.transpose(rest[:, c, :], words[:, chunks[2 + c]], ident[:])
-        u_bf[2] = pool.tile([P, P, PACK], BF16, name="u_bf2", align_bytes=64)
-        nc.scalar.copy(pair_words[0][:, 0, :], rest[:, 0, :])
-        nc.scalar.copy(words_of(2)[:, :, 0], rest[:, 1, :])
+            nc.tensor.transpose(word_banks[c][:, 0, :], first_words[:, chunks[c]], ident[:])
+        other_words = psum.tile([P, 2, P], F32, name="other_words")
+        for i in range(2):
+            nc.tensor.transpose(other_words[:, i, :], first_words[:, chunks[ON_TENSOR + i]], ident[:])
+        pairs2 = pool.tile([P, 2, P, 2], BF16, name="pairs2", align_bytes=64)
+        pairs2_words = pairs2[:].rearrange("p h n e -> p (h n e)").bitcast(F32).rearrange("p (h n) -> p h n", h=2)
+        u3 = pool.tile([P, P, PACK], BF16, name="u3", align_bytes=64)
+        nc.scalar.copy(pairs2_words[:, 0, :], other_words[:, 0, :])
+        nc.scalar.copy(as_word_pairs(u3)[:, :, 0], other_words[:, 1, :])
 
-        late_tags = ("turned", "spread")
-        late = [psum.tile([P, 2, P], F32, name=tag) for tag in late_tags]
-        late_u = [pool.tile([P, P, 2], BF16, name="late_u%d" % c, align_bytes=64) for c in range(ON_TENSOR)]
-        nc.vector.tensor_copy(tab[1][:, 1, :], c_win[1][:].indirect(pos[:]))
-        nc.vector.tensor_copy(kg[:, 2, :], k_win[3][:].indirect(tok[:]))
-        nc.gpsimd.tensor_tensor(from_odd[:, 3, :], tab[1][:, 1, :], kg[:, 2, :], ALU.mult)
-        nc.vector.tensor_copy(tab[1][:, 2, :], w_win[1][:].indirect(pos[:]))
-        nc.vector.scalar_tensor_tensor(from_odd[:, 2, :], kg[:, 2, :], -1.0, tab[1][:, 2, :], ALU.mult, ALU.mult)
+        second_sums = [psum.tile([P, 2, P], F32, name="bank%d" % c) for c in range(ON_TENSOR)]
+        second_u = [pool.tile([P, P, 2], BF16, name="stage%d" % c, align_bytes=64) for c in range(ON_TENSOR)]
+        second_tables = pool.tile([P, 2, N], F32, name="second_tables")
+        nc.vector.tensor_copy(second_tables[:, 0, :], c_win[1][:].indirect(pos[:]))
+        nc.vector.tensor_copy(keys[:, 2, :], k_win[3][:].indirect(tok[:]))
+        nc.gpsimd.tensor_tensor(from_odd[:, 3, :], second_tables[:, 0, :], keys[:, 2, :], ALU.mult)
+        nc.vector.tensor_copy(second_tables[:, 1, :], w_win[1][:].indirect(pos[:]))
+        nc.vector.scalar_tensor_tensor(from_odd[:, 2, :], keys[:, 2, :], -1.0, second_tables[:, 1, :], ALU.mult, ALU.mult)
         for j in (1, 0):
             for c in range(ON_TENSOR):
-                turn(late[c][:, j, :], from_odd, 2 + j, c, j == 1, False)
+                turn_and_add(second_sums[c][:, j, :], from_odd[:, 2 + j, chunks[c]], start=j == 1, stop=False)
 
         q_bf = pool.tile([P, NQ, PACK], BF16, name="q_bf", align_bytes=64)
-        q_codes = pool.tile([P, NQ], U32, name="q_codes", align_bytes=64)
-        q_scales = pool.tile([P, NQ], U8, name="q_scales", align_bytes=64)
-        u_scales = pool.tile([P, N], U8, name="u_scales", align_bytes=64)
-        scores = {}
-        mins = [pool.tile([P, 1], F32, name="min%d" % c) for c in range(N // P)]
-        spare = pool.tile([P, N], F32, name="spare")
+        for c in range(CHUNKS):
+            for j in range(2):
+                nc.vector.tensor_tensor(
+                    from_even[:, 2 + j, chunks[c]],
+                    k_win[2][:].indirect(tok[:, list_columns(chunks[c])]),
+                    second_tables[:, j, chunks[c]],
+                    ALU.mult,
+                )
+                if c < ON_TENSOR:
+                    turn_and_add(second_sums[c][:, j, :], from_even[:, 2 + j, chunks[c]], start=False, stop=j == 1)
+            if c == 0:
+                nc.scalar.copy(q_bf[:], q_raw[:].rearrange("p t m -> p m t"))
+            if c < ON_TENSOR:
+                nc.scalar.copy(second_u[c][:], second_sums[c][:].rearrange("s t p -> s p t"))
+                nc.tensor.transpose(
+                    word_banks[c][:, 1, :], second_u[c][:].rearrange("s p t -> s (p t)").bitcast(F32), ident[:]
+                )
+        u01 = pool.tile([P, ON_TENSOR * P, PACK], BF16, name="u01", align_bytes=64)
+        for c in range(ON_TENSOR):
+            nc.scalar.copy(as_word_pairs(u01)[:, chunks[c], :], word_banks[c][:].rearrange("p h n -> p n h"))
 
-        def leave(c):
-            nc.scalar.copy(late_u[c][:], late[c][:].rearrange("s t p -> s p t"))
-            nc.tensor.transpose(backs[c][:, 1, :], late_u[c][:].rearrange("s p t -> s (p t)").bitcast(F32), ident[:])
-
-        def join(c):
-            nc.scalar.copy(words_of(0)[:, chunks[c], :], backs[c][:].rearrange("p h n -> p n h"))
-
-        def add_pair(c):
+        def add_second_pair(target, c):
             nc.vector.tensor_tensor(
-                u_pair[0][:, 1, :, :] if c == 2 else u_bf[2][:, :, 2:PACK],
+                target,
                 from_even[:, 2:PACK, chunks[c]].rearrange("p t n -> p n t"),
                 from_odd[:, 2:PACK, chunks[c]].rearrange("p t n -> p n t"),
                 ALU.add,
             )
-            if c == 2:
-                u_bf[1] = pool.tile([P, P, PACK], BF16, name="late_u1", align_bytes=64)
-                nc.scalar.copy(words_of(1), pair_words[0].rearrange("p h n -> p n h"))
 
-        def score(i):
-            cols = runs[i]
+        add_second_pair(pairs2[:, 1, :, :], 2)
+        u2 = pool.tile([P, P, PACK], BF16, name="stage1", align_bytes=64)
+        nc.scalar.copy(as_word_pairs(u2), pairs2_words.rearrange("p h n -> p n h"))
+        add_second_pair(u3[:, :, 2:PACK], 3)
+
+        q_codes = pool.tile([P, NQ], U32, name="q_codes", align_bytes=64)
+        q_scales = pool.tile([P, NQ], U8, name="q_scales", align_bytes=64)
+        u_scales = pool.tile([P, N], U8, name="u_scales", align_bytes=64)
+        nc.vector.quantize_mx(
+            out=q_codes[:].bitcast(FP8X4), scales=q_scales[:], in_=q_bf[:].rearrange("p m t -> p (m t)")
+        )
+        scored = []
+        for i, (u, cols) in enumerate(((u3, chunks[3]), (u01, slice(0, ON_TENSOR * P)), (u2, chunks[2]))):
             width = cols.stop - cols.start
             codes = pool.tile([P, width], U32, name="codes%d" % i, align_bytes=64)
             nc.vector.quantize_mx(
-                out=codes[:].bitcast(FP8X4),
-                scales=u_scales[:, cols],
-                in_=u_bf[i][:].rearrange("p n t -> p (n t)"),
+                out=codes[:].bitcast(FP8X4), scales=u_scales[:, cols], in_=u[:].rearrange("p n t -> p (n t)")
             )
-            scores[i] = psum.tile([P, width], F32, name="scores%d" % i)
+            scores = psum.tile([P, width], F32, name="scores%d" % i)
             nc.tensor.matmul_mx(
-                out=scores[i][:],
+                out=scores[:],
                 lhsT=q_codes[:].bitcast(FP8X4),
                 lhsT_scale=q_scales[:],
                 rhs=codes[:].bitcast(FP8X4),
@@ -187,42 +187,13 @@ def tile_attend_pre_ropew_f_topk_kernel(tc, qT, kT, cT, wT, kb, offs, offs2, out
                 start=True,
                 stop=True,
             )
+            scored.append((scores, cols))
 
-        def bias(i):
-            nc.vector.tensor_tensor(neg_x[:, runs[i]], neg_b[:, runs[i]], scores[i][:], ALU.subtract)
-
-        def least(c, cols, before):
-            if before is None:
-                nc.vector.tensor_reduce(mins[c][:], neg_x[:, cols], AX.X, ALU.min)
-            else:
-                nc.vector.tensor_scalar(
-                    spare[:, cols], neg_x[:, cols], 1.0, mins[before][:], ALU.mult, ALU.min, accum_out=mins[c][:]
-                )
-
-        for c in range(N // P):
-            for j in range(2):
-                rotate(2, j, chunks[c])
-                if c < ON_TENSOR:
-                    turn(late[c][:, j, :], from_even, 2 + j, c, False, j == 1)
-            if c == 0:
-                nc.scalar.copy(q_bf[:], q_raw[:].rearrange("p t m -> p m t"))
-            if c < ON_TENSOR:
-                leave(c)
-        u_bf[0] = pool.tile([P, 2 * P, PACK], BF16, name="u_bf0", align_bytes=64)
-        join(0)
-        join(1)
-        add_pair(2)
-        add_pair(3)
-        nc.vector.quantize_mx(
-            out=q_codes[:].bitcast(FP8X4), scales=q_scales[:], in_=q_bf[:].rearrange("p m t -> p (m t)")
-        )
-        for i in (2, 0, 1):
-            score(i)
-        neg_x = pool.tile([P, N], F32, name="late_u1", align_bytes=64)
-        for i in (2, 0, 1):
-            bias(i)
-        least(3, slice(0, N), None)
-        neg_m = mins[3]
+        neg_x = pool.tile([P, N], F32, name="stage1", align_bytes=64)
+        for scores, cols in scored:
+            nc.vector.tensor_tensor(neg_x[:, cols], neg_b[:, cols], scores[:], ALU.subtract)
+        neg_m = pool.tile([P, 1], F32, name="neg_m")
+        nc.vector.tensor_reduce(neg_m[:], neg_x[:], AX.X, ALU.min)
         e = pool.tile([P, N], F32, name="e")
         total = pool.tile([P, 1], F32, name="total")
         nc.scalar.activation(e[:], neg_x[:], ACT.Exp, bias=neg_m[:], scale=-1.0, accum_out=total[:])

@@ -111,11 +111,9 @@ def tile_attend_pre_ropew_f_topk_kernel(tc, qT, kT, cT, wT, kb, offs, offs2, out
         other_words = psum.tile([P, 2, P], F32, name="other_words")
         for i in range(2):
             nc.tensor.transpose(other_words[:, i, :], first_words[:, chunks[ON_TENSOR + i]], ident[:])
-        pairs2 = pool.tile([P, 2, P, 2], BF16, name="pairs2", align_bytes=64)
-        pairs2_words = pairs2[:].rearrange("p h n e -> p (h n e)").bitcast(F32).rearrange("p (h n) -> p h n", h=2)
-        u3 = pool.tile([P, P, PACK], BF16, name="u3", align_bytes=64)
-        nc.scalar.copy(pairs2_words[:, 0, :], other_words[:, 0, :])
-        nc.scalar.copy(as_word_pairs(u3)[:, :, 0], other_words[:, 1, :])
+        u23 = [pool.tile([P, P, PACK], BF16, name="u%d" % c, align_bytes=64) for c in (2, 3)]
+        for i in range(2):
+            nc.scalar.copy(as_word_pairs(u23[i])[:, :, 0], other_words[:, i, :])
 
         second_sums = [psum.tile([P, 2, P], F32, name="bank%d" % c) for c in range(ON_TENSOR)]
         second_u = [pool.tile([P, P, 2], BF16, name="stage%d" % c, align_bytes=64) for c in range(ON_TENSOR)]
@@ -147,9 +145,9 @@ def tile_attend_pre_ropew_f_topk_kernel(tc, qT, kT, cT, wT, kb, offs, offs2, out
                 nc.tensor.transpose(
                     word_banks[c][:, 1, :], second_u[c][:].rearrange("s p t -> s (p t)").bitcast(F32), ident[:]
                 )
-        u01 = pool.tile([P, ON_TENSOR * P, PACK], BF16, name="u01", align_bytes=64)
+        u01 = [pool.tile([P, P, PACK], BF16, name="u%d" % c, align_bytes=64) for c in range(ON_TENSOR)]
         for c in range(ON_TENSOR):
-            nc.scalar.copy(as_word_pairs(u01)[:, chunks[c], :], word_banks[c][:].rearrange("p h n -> p n h"))
+            nc.scalar.copy(as_word_pairs(u01[c]), word_banks[c][:].rearrange("p h n -> p n h"))
 
         def add_second_pair(target, c):
             nc.vector.tensor_tensor(
@@ -159,10 +157,8 @@ def tile_attend_pre_ropew_f_topk_kernel(tc, qT, kT, cT, wT, kb, offs, offs2, out
                 ALU.add,
             )
 
-        add_second_pair(pairs2[:, 1, :, :], 2)
-        u2 = pool.tile([P, P, PACK], BF16, name="stage1", align_bytes=64)
-        nc.scalar.copy(as_word_pairs(u2), pairs2_words.rearrange("p h n -> p n h"))
-        add_second_pair(u3[:, :, 2:PACK], 3)
+        add_second_pair(u23[0][:, :, 2:PACK], 2)
+        add_second_pair(u23[1][:, :, 2:PACK], 3)
 
         q_codes = pool.tile([P, NQ], U32, name="q_codes", align_bytes=64)
         q_scales = pool.tile([P, NQ], U8, name="q_scales", align_bytes=64)
@@ -171,13 +167,13 @@ def tile_attend_pre_ropew_f_topk_kernel(tc, qT, kT, cT, wT, kb, offs, offs2, out
             out=q_codes[:].bitcast(FP8X4), scales=q_scales[:], in_=q_bf[:].rearrange("p m t -> p (m t)")
         )
         scored = []
-        for i, (u, cols) in enumerate(((u3, chunks[3]), (u01, slice(0, ON_TENSOR * P)), (u2, chunks[2]))):
+        for i, (u, cols) in enumerate(((u23[0], chunks[2]), (u23[1], chunks[3]), (u01[0], chunks[0]), (u01[1], chunks[1]))):
             width = cols.stop - cols.start
             codes = pool.tile([P, width], U32, name="codes%d" % i, align_bytes=64)
             nc.vector.quantize_mx(
                 out=codes[:].bitcast(FP8X4), scales=u_scales[:, cols], in_=u[:].rearrange("p n t -> p (n t)")
             )
-            scores = psum.tile([P, width], F32, name="scores%d" % i)
+            scores = psum.tile([P, width], F32, name=("scores0", "scores1", "scores2", "other_words")[i])
             nc.tensor.matmul_mx(
                 out=scores[:],
                 lhsT=q_codes[:].bitcast(FP8X4),
@@ -189,7 +185,7 @@ def tile_attend_pre_ropew_f_topk_kernel(tc, qT, kT, cT, wT, kb, offs, offs2, out
             )
             scored.append((scores, cols))
 
-        neg_x = pool.tile([P, N], F32, name="stage1", align_bytes=64)
+        neg_x = pool.tile([P, N], F32, name="u1", align_bytes=64)
         for scores, cols in scored:
             nc.vector.tensor_tensor(neg_x[:, cols], neg_b[:, cols], scores[:], ALU.subtract)
         neg_m = pool.tile([P, 1], F32, name="neg_m")

@@ -57,10 +57,10 @@ def tile_attend_pre_ropew_f_topk_kernel(tc, qT, kT, cT, wT, kb, offs, offs2, out
         nc.sync.dma_start(w_win[0][:], w_rows[0])
         for t in range(2):
             nc.sync.dma_start(k_win[t][:], k_rows[t])
-        nc.sync.dma_start(c_win[1][:], c_rows[2])
-        nc.sync.dma_start(k_win[3][:], k_rows[3])
         nc.sync.dma_start(w_win[1][:], w_rows[2])
         nc.sync.dma_start(k_win[2][:], k_rows[2])
+        nc.sync.dma_start(c_win[1][:], c_rows[2])
+        nc.sync.dma_start(k_win[3][:], k_rows[3])
         nc.sync.dma_start(q_raw[:], qT[0].rearrange("(p t) m -> p t m", t=PACK))
 
         chunks = [slice(c * P, (c + 1) * P) for c in range(CHUNKS)]
@@ -91,17 +91,26 @@ def tile_attend_pre_ropew_f_topk_kernel(tc, qT, kT, cT, wT, kb, offs, offs2, out
         word_banks = [psum.tile([P, 2, P], F32, name="words%d" % c) for c in range(ON_TENSOR)]
         first_sums = [psum.tile([P, 2, 2, P], F32, name="bank%d" % half) for half in range(2)]
         keys = pool.tile([P, 3, N], F32, name="keys")
+        halves = [slice(0, N // 2), slice(N // 2, N)]
         for t in range(2):
             term = (from_even, from_odd)[t]
-            nc.vector.tensor_copy(keys[:, t, :], k_win[t][:].indirect(tok[:]))
-            for j in range(2):
-                nc.gpsimd.tensor_tensor(term[:, j, :], first_tables[:, 1 - t + j, :], keys[:, t, :], ALU.mult)
-                for c in range(CHUNKS):
-                    half, inner = divmod(c, 2)
-                    turn_and_add(
-                        first_sums[half][:, inner, j, :], term[:, j, chunks[c]],
-                        start=(t, j, inner) == (0, 0, 0), stop=(t, j, inner) == (1, 1, 1),
-                    )
+            for half, cols in enumerate(halves):
+                nc.vector.tensor_copy(keys[:, t, cols], k_win[t][:].indirect(tok[:, list_columns(cols)]))
+                nc.gpsimd.tensor_tensor(
+                    term[:, 0:2, cols],
+                    first_tables[:, 1 - t : 3 - t, cols],
+                    keys[:, t : t + 1, cols].to_broadcast([P, 2, N // 2]),
+                    ALU.mult,
+                )
+                for j in range(2):
+                    for inner in range(2):
+                        turn_and_add(
+                            first_sums[half][:, inner, j, :], term[:, j, chunks[2 * half + inner]],
+                            start=(t, j, inner) == (0, 0, 0), stop=(t, j, inner) == (1, 1, 1),
+                        )
+        second_tables = pool.tile([P, 3, N], F32, name="second_tables")
+        nc.vector.tensor_copy(second_tables[:, 2, :], w_win[1][:].indirect(pos[:]))
+        nc.scalar.activation(second_tables[:, 0, :], second_tables[:, 2, :], ACT.Copy, scale=-1.0)
         first_u = pool.tile([P, CHUNKS, P, 2], BF16, name="first_u", align_bytes=64)
         for half in range(2):
             nc.scalar.copy(first_u[:, 2 * half : 2 * half + 2, :, :], first_sums[half][:].rearrange("s c t p -> s c p t"))
@@ -117,27 +126,28 @@ def tile_attend_pre_ropew_f_topk_kernel(tc, qT, kT, cT, wT, kb, offs, offs2, out
 
         second_sums = [psum.tile([P, 2, P], F32, name="bank%d" % c) for c in range(ON_TENSOR)]
         second_u = [pool.tile([P, P, 2], BF16, name="stage%d" % c, align_bytes=64) for c in range(ON_TENSOR)]
-        second_tables = pool.tile([P, 2, N], F32, name="second_tables")
-        nc.vector.tensor_copy(second_tables[:, 0, :], c_win[1][:].indirect(pos[:]))
-        nc.vector.tensor_copy(keys[:, 2, :], k_win[3][:].indirect(tok[:]))
-        nc.gpsimd.tensor_tensor(from_odd[:, 3, :], second_tables[:, 0, :], keys[:, 2, :], ALU.mult)
-        nc.vector.tensor_copy(second_tables[:, 1, :], w_win[1][:].indirect(pos[:]))
-        nc.vector.scalar_tensor_tensor(from_odd[:, 2, :], keys[:, 2, :], -1.0, second_tables[:, 1, :], ALU.mult, ALU.mult)
+        for cols in halves:
+            nc.vector.tensor_copy(keys[:, 2, cols], k_win[2][:].indirect(tok[:, list_columns(cols)]))
+            nc.gpsimd.tensor_tensor(from_even[:, 3, cols], second_tables[:, 2, cols], keys[:, 2, cols], ALU.mult)
+        for cols in halves:
+            nc.vector.tensor_copy(second_tables[:, 1, cols], c_win[1][:].indirect(pos[:, list_columns(cols)]))
+        for cols in halves:
+            nc.vector.tensor_tensor(from_even[:, 2, cols], keys[:, 2, cols], second_tables[:, 1, cols], ALU.mult)
         for j in (1, 0):
             for c in range(ON_TENSOR):
-                turn_and_add(second_sums[c][:, j, :], from_odd[:, 2 + j, chunks[c]], start=j == 1, stop=False)
+                turn_and_add(second_sums[c][:, j, :], from_even[:, 2 + j, chunks[c]], start=j == 1, stop=False)
 
         q_bf = pool.tile([P, NQ, PACK], BF16, name="q_bf", align_bytes=64)
         for c in range(CHUNKS):
-            for j in range(2):
+            for j in (1, 0):
                 nc.vector.tensor_tensor(
-                    from_even[:, 2 + j, chunks[c]],
-                    k_win[2][:].indirect(tok[:, list_columns(chunks[c])]),
+                    from_odd[:, 2 + j, chunks[c]],
+                    k_win[3][:].indirect(tok[:, list_columns(chunks[c])]),
                     second_tables[:, j, chunks[c]],
                     ALU.mult,
                 )
                 if c < ON_TENSOR:
-                    turn_and_add(second_sums[c][:, j, :], from_even[:, 2 + j, chunks[c]], start=False, stop=j == 1)
+                    turn_and_add(second_sums[c][:, j, :], from_odd[:, 2 + j, chunks[c]], start=False, stop=j == 0)
             if c == 0:
                 nc.scalar.copy(q_bf[:], q_raw[:].rearrange("p t m -> p m t"))
             if c < ON_TENSOR:

@@ -138,15 +138,20 @@ def tile_attend_pre_ropew_f_topk_kernel(tc, qT, kT, cT, wT, kb, offs, offs2, out
                 turn_and_add(second_sums[c][:, j, :], from_even[:, 2 + j, chunks[c]], start=j == 1, stop=False)
 
         q_bf = pool.tile([P, NQ, PACK], BF16, name="q_bf", align_bytes=64)
+        def odd_product(j, cols):
+            nc.vector.tensor_tensor(
+                from_odd[:, 2 + j, cols],
+                k_win[3][:].indirect(tok[:, list_columns(cols)]),
+                second_tables[:, j, cols],
+                ALU.mult,
+            )
+
         for c in range(CHUNKS):
-            for j in (1, 0):
-                nc.vector.tensor_tensor(
-                    from_odd[:, 2 + j, chunks[c]],
-                    k_win[3][:].indirect(tok[:, list_columns(chunks[c])]),
-                    second_tables[:, j, chunks[c]],
-                    ALU.mult,
-                )
-                if c < ON_TENSOR:
+            if c % 2 == 0:
+                odd_product(1, halves[c // 2])
+            odd_product(0, chunks[c])
+            if c < ON_TENSOR:
+                for j in (1, 0):
                     turn_and_add(second_sums[c][:, j, :], from_odd[:, 2 + j, chunks[c]], start=False, stop=j == 0)
             if c == 0:
                 nc.scalar.copy(q_bf[:], q_raw[:].rearrange("p t m -> p m t"))
@@ -206,6 +211,6 @@ def tile_attend_pre_ropew_f_topk_kernel(tc, qT, kT, cT, wT, kb, offs, offs2, out
         inv = pool.tile([P, 1], F32, name="inv")
         nc.vector.reciprocal(inv[:], total[:])
         y = pool.tile([P, N], F32, name="y")
-        for cols, queue in ((slice(0, N // 2), nc.sync), (slice(N // 2, N), nc.scalar)):
+        for cols in halves:
             nc.vector.tensor_scalar_mul(y[:, cols], e[:, cols], inv[:])
-            queue.dma_start(out[0, :, cols], y[:, cols])
+            nc.sync.dma_start(out[0, :, cols], y[:, cols])

@@ -21,6 +21,7 @@ P = 128
 PACK = 4
 CHUNKS = N // P
 ON_TENSOR = 2
+ON_SCALAR = 160
 
 
 def tile_attend_pre_ropew_f_topk_kernel(tc, qT, kT, cT, wT, kb, offs, offs2, out):
@@ -211,6 +212,7 @@ def tile_attend_pre_ropew_f_topk_kernel(tc, qT, kT, cT, wT, kb, offs, offs2, out
         inv = pool.tile([P, 1], F32, name="inv")
         nc.vector.reciprocal(inv[:], total[:])
         y = pool.tile([P, N], F32, name="y")
-        for cols in halves:
-            nc.vector.tensor_scalar_mul(y[:, cols], e[:, cols], inv[:])
-            nc.sync.dma_start(out[0, :, cols], y[:, cols])
+        first, rest = slice(0, ON_SCALAR), slice(ON_SCALAR, N)
+        nc.scalar.activation(y[:, first], e[:, first], ACT.Copy, scale=inv[:])
+        nc.vector.tensor_scalar_mul(y[:, rest], e[:, rest], inv[:])
+        nc.sync.dma_start(out[0], y[:])

@@ -39,7 +39,7 @@ def tile_attend_pre_ropew_f_topk_kernel(tc, qT, kT, cT, wT, kb, offs, offs2, out
         tok = pool.tile([P, N // 16], U16, name="tok")
         pos = pool.tile([P, N // 16], U16, name="pos")
         k_win = [pool.tile([P, T], F32, name="k_win%d" % t) for t in range(PACK)]
-        c_win = [pool.tile([P, T2], F32, name="c_win%d" % h) for h in range(2)]
+        c_win = [pool.tile([P, T2], F32, name="c_win%d" % h, align_bytes=64) for h in range(2)]
         w_win = [pool.tile([P, T2], F32, name="w_win%d" % h) for h in range(2)]
         b_win = pool.tile([P, T], F32, name="b_win")
         q_raw = pool.tile([P, PACK, NQ], F32, name="q_raw")
@@ -91,13 +91,13 @@ def tile_attend_pre_ropew_f_topk_kernel(tc, qT, kT, cT, wT, kb, offs, offs2, out
 
         word_banks = [psum.tile([P, 2, P], F32, name="words%d" % c) for c in range(ON_TENSOR)]
         first_sums = [psum.tile([P, 2, 2, P], F32, name="bank%d" % half) for half in range(2)]
-        keys = pool.tile([P, 3, N], F32, name="keys")
+        keys = pool.tile([P, 2, N], F32, name="keys")
         halves = [slice(0, N // 2), slice(N // 2, N)]
         for t in range(2):
             term = (from_even, from_odd)[t]
             for half, cols in enumerate(halves):
                 nc.vector.tensor_copy(keys[:, t, cols], k_win[t][:].indirect(tok[:, list_columns(cols)]))
-                nc.gpsimd.tensor_tensor(
+                (nc.gpsimd, nc.vector)[t].tensor_tensor(
                     term[:, 0:2, cols],
                     first_tables[:, 1 - t : 3 - t, cols],
                     keys[:, t : t + 1, cols].to_broadcast([P, 2, N // 2]),
@@ -109,9 +109,10 @@ def tile_attend_pre_ropew_f_topk_kernel(tc, qT, kT, cT, wT, kb, offs, offs2, out
                             first_sums[half][:, inner, j, :], term[:, j, chunks[2 * half + inner]],
                             start=(t, j, inner) == (0, 0, 0), stop=(t, j, inner) == (1, 1, 1),
                         )
-        second_tables = pool.tile([P, 3, N], F32, name="second_tables")
-        nc.vector.tensor_copy(second_tables[:, 2, :], w_win[1][:].indirect(pos[:]))
-        nc.scalar.activation(second_tables[:, 0, :], second_tables[:, 2, :], ACT.Copy, scale=-1.0)
+        second_tables = pool.tile([P, 3, N], F32, name="k_win1")
+        nc.scalar.activation(second_tables[:, 2, :], w_win[1][:].indirect(pos[:]), ACT.Copy)
+        nc.vector.tensor_scalar_mul(second_tables[:, 0, :], second_tables[:, 2, :], -1.0)
+        even_keys = pool.tile([P, N], F32, name="w_win1")
         first_u = pool.tile([P, CHUNKS, P, 2], BF16, name="first_u", align_bytes=64)
         for half in range(2):
             nc.scalar.copy(first_u[:, 2 * half : 2 * half + 2, :, :], first_sums[half][:].rearrange("s c t p -> s c p t"))
@@ -128,39 +129,46 @@ def tile_attend_pre_ropew_f_topk_kernel(tc, qT, kT, cT, wT, kb, offs, offs2, out
         second_sums = [psum.tile([P, 2, P], F32, name="bank%d" % c) for c in range(ON_TENSOR)]
         second_u = [pool.tile([P, P, 2], BF16, name="stage%d" % c, align_bytes=64) for c in range(ON_TENSOR)]
         for cols in halves:
-            nc.vector.tensor_copy(keys[:, 2, cols], k_win[2][:].indirect(tok[:, list_columns(cols)]))
-            nc.gpsimd.tensor_tensor(from_even[:, 3, cols], second_tables[:, 2, cols], keys[:, 2, cols], ALU.mult)
+            nc.vector.tensor_copy(even_keys[:, cols], k_win[2][:].indirect(tok[:, list_columns(cols)]))
+            nc.gpsimd.tensor_tensor(from_even[:, 3, cols], second_tables[:, 2, cols], even_keys[:, cols], ALU.mult)
         for cols in halves:
             nc.vector.tensor_copy(second_tables[:, 1, cols], c_win[1][:].indirect(pos[:, list_columns(cols)]))
         for cols in halves:
-            nc.vector.tensor_tensor(from_even[:, 2, cols], keys[:, 2, cols], second_tables[:, 1, cols], ALU.mult)
+            nc.vector.tensor_tensor(from_even[:, 2, cols], even_keys[:, cols], second_tables[:, 1, cols], ALU.mult)
         for j in (1, 0):
             for c in range(ON_TENSOR):
                 turn_and_add(second_sums[c][:, j, :], from_even[:, 2 + j, chunks[c]], start=j == 1, stop=False)
 
-        q_bf = pool.tile([P, NQ, PACK], BF16, name="q_bf", align_bytes=64)
-        def odd_product(j, cols):
+        last_keys = pool.tile([P, N], F32, name="first_u", align_bytes=64)
+        for cols in (chunks[1], halves[1]):
+            nc.scalar.activation(last_keys[:, cols], k_win[3][:].indirect(tok[:, list_columns(cols)]), ACT.Copy)
+        for j in (1, 0):
             nc.vector.tensor_tensor(
-                from_odd[:, 2 + j, cols],
-                k_win[3][:].indirect(tok[:, list_columns(cols)]),
-                second_tables[:, j, cols],
+                from_odd[:, 2 + j, chunks[0]],
+                k_win[3][:].indirect(tok[:, list_columns(chunks[0])]),
+                second_tables[:, j, chunks[0]],
                 ALU.mult,
             )
 
-        for c in range(CHUNKS):
-            if c % 2 == 0:
-                odd_product(1, halves[c // 2])
-            odd_product(0, chunks[c])
-            if c < ON_TENSOR:
-                for j in (1, 0):
-                    turn_and_add(second_sums[c][:, j, :], from_odd[:, 2 + j, chunks[c]], start=False, stop=j == 0)
-            if c == 0:
-                nc.scalar.copy(q_bf[:], q_raw[:].rearrange("p t m -> p m t"))
-            if c < ON_TENSOR:
-                nc.scalar.copy(second_u[c][:], second_sums[c][:].rearrange("s t p -> s p t"))
-                nc.tensor.transpose(
-                    word_banks[c][:, 1, :], second_u[c][:].rearrange("s p t -> s (p t)").bitcast(F32), ident[:]
-                )
+        def odd_products(cols):
+            nc.vector.tensor_tensor(
+                from_odd[:, 2:PACK, cols],
+                second_tables[:, 0:2, cols],
+                last_keys[:, cols].unsqueeze(1).to_broadcast([P, 2, cols.stop - cols.start]),
+                ALU.mult,
+            )
+
+        odd_products(chunks[1])
+        q_bf = pool.tile([P, NQ, PACK], BF16, name="c_win1", align_bytes=64)
+        nc.vector.tensor_copy(q_bf[:], q_raw[:].rearrange("p t m -> p m t"))
+        odd_products(halves[1])
+        for c in range(ON_TENSOR):
+            for j in (1, 0):
+                turn_and_add(second_sums[c][:, j, :], from_odd[:, 2 + j, chunks[c]], start=False, stop=j == 0)
+            nc.scalar.copy(second_u[c][:], second_sums[c][:].rearrange("s t p -> s p t"))
+            nc.tensor.transpose(
+                word_banks[c][:, 1, :], second_u[c][:].rearrange("s p t -> s (p t)").bitcast(F32), ident[:]
+            )
         u01 = [pool.tile([P, P, PACK], BF16, name="u%d" % c, align_bytes=64) for c in range(ON_TENSOR)]
         for c in range(ON_TENSOR):
             nc.scalar.copy(as_word_pairs(u01[c]), word_banks[c][:].rearrange("p h n -> p n h"))

@@ -139,29 +139,23 @@ def tile_attend_pre_ropew_f_topk_kernel(tc, qT, kT, cT, wT, kb, offs, offs2, out
             for c in range(ON_TENSOR):
                 turn_and_add(second_sums[c][:, j, :], from_even[:, 2 + j, chunks[c]], start=j == 1, stop=False)
 
-        last_keys = pool.tile([P, N], F32, name="first_u", align_bytes=64)
-        for cols in (chunks[1], halves[1]):
-            nc.scalar.activation(last_keys[:, cols], k_win[3][:].indirect(tok[:, list_columns(cols)]), ACT.Copy)
-        for j in (1, 0):
+        last_keys = pool.tile([P, 1, N // 2], F32, name="first_u", align_bytes=64)
+        nc.scalar.activation(last_keys[:, 0, :], k_win[3][:].indirect(tok[:, list_columns(halves[1])]), ACT.Copy)
+        for j, cols in ((1, halves[0]), (0, chunks[0]), (0, chunks[1])):
             nc.vector.tensor_tensor(
-                from_odd[:, 2 + j, chunks[0]],
-                k_win[3][:].indirect(tok[:, list_columns(chunks[0])]),
-                second_tables[:, j, chunks[0]],
+                from_odd[:, 2 + j, cols],
+                k_win[3][:].indirect(tok[:, list_columns(cols)]),
+                second_tables[:, j, cols],
                 ALU.mult,
             )
-
-        def odd_products(cols):
-            nc.vector.tensor_tensor(
-                from_odd[:, 2:PACK, cols],
-                second_tables[:, 0:2, cols],
-                last_keys[:, cols].unsqueeze(1).to_broadcast([P, 2, cols.stop - cols.start]),
-                ALU.mult,
-            )
-
-        odd_products(chunks[1])
+        nc.vector.tensor_tensor(
+            from_odd[:, 2:PACK, halves[1]],
+            second_tables[:, 0:2, halves[1]],
+            last_keys[:].to_broadcast([P, 2, N // 2]),
+            ALU.mult,
+        )
         q_bf = pool.tile([P, NQ, PACK], BF16, name="c_win1", align_bytes=64)
-        nc.vector.tensor_copy(q_bf[:], q_raw[:].rearrange("p t m -> p m t"))
-        odd_products(halves[1])
+        nc.scalar.copy(q_bf[:], q_raw[:].rearrange("p t m -> p m t"))
         for c in range(ON_TENSOR):
             for j in (1, 0):
                 turn_and_add(second_sums[c][:, j, :], from_odd[:, 2 + j, chunks[c]], start=False, stop=j == 0)

@@ -28,6 +28,7 @@ def tile_attend_pre_ropew_f_topk_kernel(tc, qT, kT, cT, wT, kb, offs, offs2, out
     nc = tc.nc
     with ExitStack() as ctx:
         pool = ctx.enter_context(tc.tile_pool(name="held", bufs=1))
+        reused = ctx.enter_context(tc.tile_pool(name="reused", bufs=1))
         psum = ctx.enter_context(tc.psum_pool(name="psum", bufs=1))
 
         def list_columns(cols):
@@ -39,7 +40,7 @@ def tile_attend_pre_ropew_f_topk_kernel(tc, qT, kT, cT, wT, kb, offs, offs2, out
         tok = pool.tile([P, N // 16], U16, name="tok")
         pos = pool.tile([P, N // 16], U16, name="pos")
         k_win = [pool.tile([P, T], F32, name="k_win%d" % t) for t in range(PACK)]
-        c_win = [pool.tile([P, T2], F32, name="c_win%d" % h, align_bytes=64) for h in range(2)]
+        c_win = [pool.tile([P, T2], F32, name="c_win0"), reused.tile([P, T2], F32, name="c_win1", offset=0)]
         w_win = [pool.tile([P, T2], F32, name="w_win%d" % h) for h in range(2)]
         b_win = pool.tile([P, T], F32, name="b_win")
         q_raw = pool.tile([P, PACK, NQ], F32, name="q_raw")
@@ -90,12 +91,12 @@ def tile_attend_pre_ropew_f_topk_kernel(tc, qT, kT, cT, wT, kb, offs, offs2, out
             nc.tensor.matmul(target, term, ident[:], start=start, stop=stop, is_transpose=True)
 
         word_banks = [psum.tile([P, 2, P], F32, name="words%d" % c) for c in range(ON_TENSOR)]
-        first_sums = [psum.tile([P, 2, 2, P], F32, name="bank%d" % half) for half in range(2)]
+        first_sums = psum.tile([P, ON_TENSOR, 2, P], F32, name="scores3")
         keys = pool.tile([P, 2, N], F32, name="keys")
         halves = [slice(0, N // 2), slice(N // 2, N)]
         for t in range(2):
             term = (from_even, from_odd)[t]
-            for half, cols in enumerate(halves):
+            for cols in halves:
                 nc.vector.tensor_copy(keys[:, t, cols], k_win[t][:].indirect(tok[:, list_columns(cols)]))
                 (nc.gpsimd, nc.vector)[t].tensor_tensor(
                     term[:, 0:2, cols],
@@ -103,43 +104,56 @@ def tile_attend_pre_ropew_f_topk_kernel(tc, qT, kT, cT, wT, kb, offs, offs2, out
                     keys[:, t : t + 1, cols].to_broadcast([P, 2, N // 2]),
                     ALU.mult,
                 )
-                for j in range(2):
-                    for inner in range(2):
-                        turn_and_add(
-                            first_sums[half][:, inner, j, :], term[:, j, chunks[2 * half + inner]],
-                            start=(t, j, inner) == (0, 0, 0), stop=(t, j, inner) == (1, 1, 1),
-                        )
+            for j in range(2):
+                for c in range(ON_TENSOR):
+                    turn_and_add(
+                        first_sums[:, c, j, :], term[:, j, chunks[c]],
+                        start=(t, j, c) == (0, 0, 0), stop=(t, j, c) == (1, 1, ON_TENSOR - 1),
+                    )
+
+        def add_pair(target, h, c):
+            places = slice(2 * h, 2 * h + 2)
+            nc.vector.tensor_tensor(
+                target[:, :, places],
+                from_even[:, places, chunks[c]].rearrange("p t n -> p n t"),
+                from_odd[:, places, chunks[c]].rearrange("p t n -> p n t"),
+                ALU.add,
+            )
+
+        u23 = [pool.tile([P, P, PACK], BF16, name="u%d" % c, align_bytes=64) for c in (2, 3)]
+        for i in range(2):
+            add_pair(u23[i], 0, ON_TENSOR + i)
         second_tables = pool.tile([P, 3, N], F32, name="k_win1")
         nc.scalar.activation(second_tables[:, 2, :], w_win[1][:].indirect(pos[:]), ACT.Copy)
-        nc.vector.tensor_scalar_mul(second_tables[:, 0, :], second_tables[:, 2, :], -1.0)
-        even_keys = pool.tile([P, N], F32, name="w_win1")
-        first_u = pool.tile([P, CHUNKS, P, 2], BF16, name="first_u", align_bytes=64)
-        for half in range(2):
-            nc.scalar.copy(first_u[:, 2 * half : 2 * half + 2, :, :], first_sums[half][:].rearrange("s c t p -> s c p t"))
+        nc.scalar.activation(second_tables[:, 0, :], second_tables[:, 2, :], ACT.Copy, scale=-1.0)
+        even_keys = pool.tile([P, 1, N], F32, name="w_win1")
+
+        second_u = [pool.tile([P, P, 2], BF16, name="stage%d" % c, align_bytes=64) for c in range(ON_TENSOR)]
+        first, second = halves
+        nc.vector.tensor_copy(even_keys[:, 0, first], k_win[2][:].indirect(tok[:, list_columns(first)]))
+        nc.scalar.activation(even_keys[:, 0, second], k_win[2][:].indirect(tok[:, list_columns(second)]), ACT.Copy)
+        nc.gpsimd.tensor_tensor(from_even[:, 3, first], second_tables[:, 2, first], even_keys[:, 0, first], ALU.mult)
+        nc.vector.tensor_copy(second_tables[:, 1, first], c_win[1][:].indirect(pos[:, list_columns(first)]))
+        nc.scalar.activation(second_tables[:, 1, second], c_win[1][:].indirect(pos[:, list_columns(second)]), ACT.Copy)
+        nc.vector.tensor_tensor(
+            from_even[:, 2:PACK, second],
+            second_tables[:, 1:3, second],
+            even_keys[:, :, second].to_broadcast([P, 2, N // 2]),
+            ALU.mult,
+        )
+        nc.vector.tensor_tensor(from_even[:, 2, first], even_keys[:, 0, first], second_tables[:, 1, first], ALU.mult)
+        first_u = reused.tile([P, ON_TENSOR, P, 2], BF16, name="first_u", offset=0)
+        nc.scalar.copy(first_u[:], first_sums[:].rearrange("s c t p -> s c p t"))
         first_words = first_u[:].rearrange("s c p t -> s (c p t)").bitcast(F32)
         for c in range(ON_TENSOR):
             nc.tensor.transpose(word_banks[c][:, 0, :], first_words[:, chunks[c]], ident[:])
-        other_words = psum.tile([P, 2, P], F32, name="other_words")
-        for i in range(2):
-            nc.tensor.transpose(other_words[:, i, :], first_words[:, chunks[ON_TENSOR + i]], ident[:])
-        u23 = [pool.tile([P, P, PACK], BF16, name="u%d" % c, align_bytes=64) for c in (2, 3)]
-        for i in range(2):
-            nc.scalar.copy(as_word_pairs(u23[i])[:, :, 0], other_words[:, i, :])
 
         second_sums = [psum.tile([P, 2, P], F32, name="bank%d" % c) for c in range(ON_TENSOR)]
-        second_u = [pool.tile([P, P, 2], BF16, name="stage%d" % c, align_bytes=64) for c in range(ON_TENSOR)]
-        for cols in halves:
-            nc.vector.tensor_copy(even_keys[:, cols], k_win[2][:].indirect(tok[:, list_columns(cols)]))
-            nc.gpsimd.tensor_tensor(from_even[:, 3, cols], second_tables[:, 2, cols], even_keys[:, cols], ALU.mult)
-        for cols in halves:
-            nc.vector.tensor_copy(second_tables[:, 1, cols], c_win[1][:].indirect(pos[:, list_columns(cols)]))
-        for cols in halves:
-            nc.vector.tensor_tensor(from_even[:, 2, cols], even_keys[:, cols], second_tables[:, 1, cols], ALU.mult)
         for j in (1, 0):
             for c in range(ON_TENSOR):
                 turn_and_add(second_sums[c][:, j, :], from_even[:, 2 + j, chunks[c]], start=j == 1, stop=False)
 
-        last_keys = pool.tile([P, 1, N // 2], F32, name="first_u", align_bytes=64)
+        last_keys = reused.tile([P, 1, N // 2], F32, name="last_keys", offset=1024)
         nc.scalar.activation(last_keys[:, 0, :], k_win[3][:].indirect(tok[:, list_columns(halves[1])]), ACT.Copy)
         for j, cols in ((1, halves[0]), (0, chunks[0]), (0, chunks[1])):
             nc.vector.tensor_tensor(
@@ -154,7 +168,7 @@ def tile_attend_pre_ropew_f_topk_kernel(tc, qT, kT, cT, wT, kb, offs, offs2, out
             last_keys[:].to_broadcast([P, 2, N // 2]),
             ALU.mult,
         )
-        q_bf = pool.tile([P, NQ, PACK], BF16, name="c_win1", align_bytes=64)
+        q_bf = reused.tile([P, NQ, PACK], BF16, name="q_bf", align_bytes=64, offset=2048)
         nc.scalar.copy(q_bf[:], q_raw[:].rearrange("p t m -> p m t"))
         for c in range(ON_TENSOR):
             for j in (1, 0):
@@ -167,16 +181,8 @@ def tile_attend_pre_ropew_f_topk_kernel(tc, qT, kT, cT, wT, kb, offs, offs2, out
         for c in range(ON_TENSOR):
             nc.scalar.copy(as_word_pairs(u01[c]), word_banks[c][:].rearrange("p h n -> p n h"))
 
-        def add_second_pair(target, c):
-            nc.vector.tensor_tensor(
-                target,
-                from_even[:, 2:PACK, chunks[c]].rearrange("p t n -> p n t"),
-                from_odd[:, 2:PACK, chunks[c]].rearrange("p t n -> p n t"),
-                ALU.add,
-            )
-
-        add_second_pair(u23[0][:, :, 2:PACK], 2)
-        add_second_pair(u23[1][:, :, 2:PACK], 3)
+        for i in range(2):
+            add_pair(u23[i], 1, ON_TENSOR + i)
 
         q_codes = pool.tile([P, NQ], U32, name="q_codes", align_bytes=64)
         q_scales = pool.tile([P, NQ], U8, name="q_scales", align_bytes=64)
@@ -191,7 +197,7 @@ def tile_attend_pre_ropew_f_topk_kernel(tc, qT, kT, cT, wT, kb, offs, offs2, out
             nc.vector.quantize_mx(
                 out=codes[:].bitcast(FP8X4), scales=u_scales[:, cols], in_=u[:].rearrange("p n t -> p (n t)")
             )
-            scores = psum.tile([P, width], F32, name=("scores0", "scores1", "scores2", "other_words")[i])
+            scores = psum.tile([P, width], F32, name=("scores0", "scores1", "scores2", "scores3")[i])
             nc.tensor.matmul_mx(
                 out=scores[:],
                 lhsT=q_codes[:].bitcast(FP8X4),

@@ -22,6 +22,7 @@ PACK = 4
 CHUNKS = N // P
 ON_TENSOR = 2
 ON_SCALAR = 160
+DMA_ALIGN = 512
 
 
 def tile_attend_pre_ropew_f_topk_kernel(tc, qT, kT, cT, wT, kb, offs, offs2, out):
@@ -39,11 +40,14 @@ def tile_attend_pre_ropew_f_topk_kernel(tc, qT, kT, cT, wT, kb, offs, offs2, out
 
         tok = pool.tile([P, N // 16], U16, name="tok")
         pos = pool.tile([P, N // 16], U16, name="pos")
-        k_win = [pool.tile([P, T], F32, name="k_win%d" % t) for t in range(PACK)]
-        c_win = [pool.tile([P, T2], F32, name="c_win0"), reused.tile([P, T2], F32, name="c_win1", offset=0)]
-        w_win = [pool.tile([P, T2], F32, name="w_win%d" % h) for h in range(2)]
-        b_win = pool.tile([P, T], F32, name="b_win")
-        q_raw = pool.tile([P, PACK, NQ], F32, name="q_raw")
+        k_win = [pool.tile([P, T], F32, name="k_win%d" % t, align_bytes=DMA_ALIGN) for t in range(PACK)]
+        c_win = [
+            pool.tile([P, T2], F32, name="c_win0", align_bytes=DMA_ALIGN),
+            reused.tile([P, T2], F32, name="c_win1", align_bytes=DMA_ALIGN, offset=0),
+        ]
+        w_win = [pool.tile([P, T2], F32, name="w_win%d" % h, align_bytes=DMA_ALIGN) for h in range(2)]
+        b_win = pool.tile([P, T], F32, name="b_win", align_bytes=DMA_ALIGN)
+        q_raw = pool.tile([P, PACK, NQ], F32, name="q_raw", align_bytes=DMA_ALIGN)
 
         k_rows = kT.rearrange("(p t) n -> t p n", t=PACK)
         c_rows = cT.rearrange("(p t) n -> t p n", t=PACK)
@@ -123,10 +127,10 @@ def tile_attend_pre_ropew_f_topk_kernel(tc, qT, kT, cT, wT, kb, offs, offs2, out
         u23 = [pool.tile([P, P, PACK], BF16, name="u%d" % c, align_bytes=64) for c in (2, 3)]
         for i in range(2):
             add_pair(u23[i], 0, ON_TENSOR + i)
-        second_tables = pool.tile([P, 3, N], F32, name="k_win1")
+        second_tables = pool.tile([P, 3, N], F32, name="k_win1", align_bytes=DMA_ALIGN)
         nc.scalar.activation(second_tables[:, 2, :], w_win[1][:].indirect(pos[:]), ACT.Copy)
         nc.scalar.activation(second_tables[:, 0, :], second_tables[:, 2, :], ACT.Copy, scale=-1.0)
-        even_keys = pool.tile([P, 1, N], F32, name="w_win1")
+        even_keys = pool.tile([P, 1, N], F32, name="w_win1", align_bytes=DMA_ALIGN)
 
         second_u = [pool.tile([P, P, 2], BF16, name="stage%d" % c, align_bytes=64) for c in range(ON_TENSOR)]
         first, second = halves
@@ -219,7 +223,7 @@ def tile_attend_pre_ropew_f_topk_kernel(tc, qT, kT, cT, wT, kb, offs, offs2, out
         nc.scalar.activation(e[:], neg_x[:], ACT.Exp, bias=neg_m[:], scale=-1.0, accum_out=total[:])
         inv = pool.tile([P, 1], F32, name="inv")
         nc.vector.reciprocal(inv[:], total[:])
-        y = pool.tile([P, N], F32, name="y")
+        y = pool.tile([P, N], F32, name="y", align_bytes=DMA_ALIGN)
         first, rest = slice(0, ON_SCALAR), slice(ON_SCALAR, N)
         nc.scalar.activation(y[:, first], e[:, first], ACT.Copy, scale=inv[:])
         nc.vector.tensor_scalar_mul(y[:, rest], e[:, rest], inv[:])

from contextlib import ExitStack

import concourse.mybir as mybir
from concourse.masks import make_identity

N, T, T2, D, NQ = 512, 2048, 1024, 512, 128
FLOPS = 2 * NQ * N * D
BYTES = 4 * (D * NQ + D * T + D * T2 + T + NQ * N) + 2 * 2 * 128 * (N // 16)

F32 = mybir.dt.float32
BF16 = mybir.dt.bfloat16
U32 = mybir.dt.uint32
U16 = mybir.dt.uint16
U8 = mybir.dt.uint8
FP8X4 = mybir.dt.float8_e4m3fn_x4
ALU = mybir.AluOpType
ACT = mybir.ActivationFunctionType
AX = mybir.AxisListType

P = 128
PACK = 4
CHUNKS = N // P
ON_TENSOR = 2
ON_SCALAR = 160
DMA_ALIGN = 512


def tile_attend_pre_ropew_f_topk_kernel(tc, qT, kT, cT, wT, kb, offs, offs2, out):
    nc = tc.nc
    with ExitStack() as ctx:
        pool = ctx.enter_context(tc.tile_pool(name="held", bufs=1))
        reused = ctx.enter_context(tc.tile_pool(name="reused", bufs=1))
        psum = ctx.enter_context(tc.psum_pool(name="psum", bufs=1))

        def list_columns(cols):
            return slice(cols.start // 16, cols.stop // 16)

        def as_word_pairs(interleaved):
            return interleaved[:].rearrange("p n t -> p (n t)").bitcast(F32).rearrange("p (n h) -> p n h", h=2)

        tok = pool.tile([P, N // 16], U16, name="tok")
        pos = pool.tile([P, N // 16], U16, name="pos")
        k_win = [pool.tile([P, T], F32, name="k_win%d" % t, align_bytes=DMA_ALIGN) for t in range(PACK)]
        c_win = [
            pool.tile([P, T2], F32, name="c_win0", align_bytes=DMA_ALIGN),
            reused.tile([P, T2], F32, name="c_win1", align_bytes=DMA_ALIGN, offset=0),
        ]
        w_win = [pool.tile([P, T2], F32, name="w_win%d" % h, align_bytes=DMA_ALIGN) for h in range(2)]
        b_win = pool.tile([P, T], F32, name="b_win", align_bytes=DMA_ALIGN)
        q_raw = pool.tile([P, PACK, NQ], F32, name="q_raw", align_bytes=DMA_ALIGN)

        k_rows = kT.rearrange("(p t) n -> t p n", t=PACK)
        c_rows = cT.rearrange("(p t) n -> t p n", t=PACK)
        w_rows = wT.rearrange("(p t) n -> t p n", t=PACK)

        nc.sync.dma_start(c_win[0][:], c_rows[0])
        nc.sync.dma_start(pos[:], offs2)
        nc.sync.dma_start(tok[:], offs)
        nc.sync.dma_start(b_win[P - 1 : P, :], kb[0:1, :])
        nc.vector.memset(b_win[0 : P - 1, :], 0.0)
        ident = pool.tile([P, P], F32, name="ident")
        make_identity(nc, ident[:])
        nc.sync.dma_start(w_win[0][:], w_rows[0])
        for t in range(2):
            nc.sync.dma_start(k_win[t][:], k_rows[t])
        nc.sync.dma_start(w_win[1][:], w_rows[2])
        nc.sync.dma_start(k_win[2][:], k_rows[2])
        nc.sync.dma_start(c_win[1][:], c_rows[2])
        nc.sync.dma_start(k_win[3][:], k_rows[3])
        nc.sync.dma_start(q_raw[:], qT[0].rearrange("(p t) m -> p t m", t=PACK))

        chunks = [slice(c * P, (c + 1) * P) for c in range(CHUNKS)]
        from_even = pool.tile([P, PACK, N], F32, name="from_even")
        from_odd = pool.tile([P, PACK, N], F32, name="from_odd")

        first_tables = pool.tile([P, 3, N], F32, name="first_tables")
        nc.vector.tensor_copy(first_tables[:, 1, :], c_win[0][:].indirect(pos[:]))
        nc.vector.tensor_copy(first_tables[:, 2, :], w_win[0][:].indirect(pos[:]))
        nc.scalar.activation(first_tables[:, 0, :], first_tables[:, 2, :], ACT.Copy, scale=-1.0)

        b_row = pool.tile([P, N], F32, name="b_row")
        b_col = pool.tile([P, CHUNKS], F32, name="b_col")
        neg_b = pool.tile([P, N], F32, name="neg_b")
        nc.vector.tensor_copy(b_row[:], b_win[:].indirect(tok[:]))
        b_turned = psum.tile([P, CHUNKS, P], F32, name="bank0")
        for c in range(CHUNKS):
            nc.tensor.transpose(b_turned[:, c, :], b_row[:, chunks[c]], ident[:])
        nc.scalar.activation(b_col[:], b_turned[:, :, P - 1], ACT.Copy, scale=-1.0)
        b_spread = psum.tile([P, N], F32, name="bank1")
        for c in range(CHUNKS):
            nc.tensor.transpose(b_spread[:, chunks[c]], b_col[:, c : c + 1].to_broadcast([P, P]), ident[:])
        nc.scalar.copy(neg_b[:], b_spread[:])

        def turn_and_add(target, term, start, stop):
            nc.tensor.matmul(target, term, ident[:], start=start, stop=stop, is_transpose=True)

        word_banks = [psum.tile([P, 2, P], F32, name="words%d" % c) for c in range(ON_TENSOR)]
        first_sums = psum.tile([P, ON_TENSOR, 2, P], F32, name="scores3")
        keys = pool.tile([P, 2, N], F32, name="keys")
        halves = [slice(0, N // 2), slice(N // 2, N)]
        for t in range(2):
            term = (from_even, from_odd)[t]
            for cols in halves:
                nc.vector.tensor_copy(keys[:, t, cols], k_win[t][:].indirect(tok[:, list_columns(cols)]))
                (nc.gpsimd, nc.vector)[t].tensor_tensor(
                    term[:, 0:2, cols],
                    first_tables[:, 1 - t : 3 - t, cols],
                    keys[:, t : t + 1, cols].to_broadcast([P, 2, N // 2]),
                    ALU.mult,
                )
            for j in range(2):
                for c in range(ON_TENSOR):
                    turn_and_add(
                        first_sums[:, c, j, :], term[:, j, chunks[c]],
                        start=(t, j, c) == (0, 0, 0), stop=(t, j, c) == (1, 1, ON_TENSOR - 1),
                    )

        def add_pair(target, h, c):
            places = slice(2 * h, 2 * h + 2)
            nc.vector.tensor_tensor(
                target[:, :, places],
                from_even[:, places, chunks[c]].rearrange("p t n -> p n t"),
                from_odd[:, places, chunks[c]].rearrange("p t n -> p n t"),
                ALU.add,
            )

        u23 = [pool.tile([P, P, PACK], BF16, name="u%d" % c, align_bytes=64) for c in (2, 3)]
        for i in range(2):
            add_pair(u23[i], 0, ON_TENSOR + i)
        second_tables = pool.tile([P, 3, N], F32, name="k_win1", align_bytes=DMA_ALIGN)
        nc.scalar.activation(second_tables[:, 2, :], w_win[1][:].indirect(pos[:]), ACT.Copy)
        nc.scalar.activation(second_tables[:, 0, :], second_tables[:, 2, :], ACT.Copy, scale=-1.0)
        even_keys = pool.tile([P, 1, N], F32, name="w_win1", align_bytes=DMA_ALIGN)

        second_u = [pool.tile([P, P, 2], BF16, name="stage%d" % c, align_bytes=64) for c in range(ON_TENSOR)]
        first, second = halves
        nc.vector.tensor_copy(even_keys[:, 0, first], k_win[2][:].indirect(tok[:, list_columns(first)]))
        nc.scalar.activation(even_keys[:, 0, second], k_win[2][:].indirect(tok[:, list_columns(second)]), ACT.Copy)
        nc.gpsimd.tensor_tensor(from_even[:, 3, first], second_tables[:, 2, first], even_keys[:, 0, first], ALU.mult)
        nc.vector.tensor_copy(second_tables[:, 1, first], c_win[1][:].indirect(pos[:, list_columns(first)]))
        nc.scalar.activation(second_tables[:, 1, second], c_win[1][:].indirect(pos[:, list_columns(second)]), ACT.Copy)
        nc.vector.tensor_tensor(
            from_even[:, 2:PACK, second],
            second_tables[:, 1:3, second],
            even_keys[:, :, second].to_broadcast([P, 2, N // 2]),
            ALU.mult,
        )
        nc.vector.tensor_tensor(from_even[:, 2, first], even_keys[:, 0, first], second_tables[:, 1, first], ALU.mult)
        first_u = reused.tile([P, ON_TENSOR, P, 2], BF16, name="first_u", offset=0)
        nc.scalar.copy(first_u[:], first_sums[:].rearrange("s c t p -> s c p t"))
        first_words = first_u[:].rearrange("s c p t -> s (c p t)").bitcast(F32)
        for c in range(ON_TENSOR):
            nc.tensor.transpose(word_banks[c][:, 0, :], first_words[:, chunks[c]], ident[:])

        second_sums = [psum.tile([P, 2, P], F32, name="bank%d" % c) for c in range(ON_TENSOR)]
        for j in (1, 0):
            for c in range(ON_TENSOR):
                turn_and_add(second_sums[c][:, j, :], from_even[:, 2 + j, chunks[c]], start=j == 1, stop=False)

        last_keys = reused.tile([P, 1, N // 2], F32, name="last_keys", offset=1024)
        nc.scalar.activation(last_keys[:, 0, :], k_win[3][:].indirect(tok[:, list_columns(halves[1])]), ACT.Copy)
        for j, cols in ((1, halves[0]), (0, chunks[0]), (0, chunks[1])):
            nc.vector.tensor_tensor(
                from_odd[:, 2 + j, cols],
                k_win[3][:].indirect(tok[:, list_columns(cols)]),
                second_tables[:, j, cols],
                ALU.mult,
            )
        nc.vector.tensor_tensor(
            from_odd[:, 2:PACK, halves[1]],
            second_tables[:, 0:2, halves[1]],
            last_keys[:].to_broadcast([P, 2, N // 2]),
            ALU.mult,
        )
        q_bf = reused.tile([P, NQ, PACK], BF16, name="q_bf", align_bytes=64, offset=2048)
        nc.scalar.copy(q_bf[:], q_raw[:].rearrange("p t m -> p m t"))
        for c in range(ON_TENSOR):
            for j in (1, 0):
                turn_and_add(second_sums[c][:, j, :], from_odd[:, 2 + j, chunks[c]], start=False, stop=j == 0)
            nc.scalar.copy(second_u[c][:], second_sums[c][:].rearrange("s t p -> s p t"))
            nc.tensor.transpose(
                word_banks[c][:, 1, :], second_u[c][:].rearrange("s p t -> s (p t)").bitcast(F32), ident[:]
            )
        u01 = [pool.tile([P, P, PACK], BF16, name="u%d" % c, align_bytes=64) for c in range(ON_TENSOR)]
        for c in range(ON_TENSOR):
            nc.scalar.copy(as_word_pairs(u01[c]), word_banks[c][:].rearrange("p h n -> p n h"))

        for i in range(2):
            add_pair(u23[i], 1, ON_TENSOR + i)

        q_codes = pool.tile([P, NQ], U32, name="q_codes", align_bytes=64)
        q_scales = pool.tile([P, NQ], U8, name="q_scales", align_bytes=64)
        u_scales = pool.tile([P, N], U8, name="u_scales", align_bytes=64)
        nc.vector.quantize_mx(
            out=q_codes[:].bitcast(FP8X4), scales=q_scales[:], in_=q_bf[:].rearrange("p m t -> p (m t)")
        )
        scored = []
        for i, (u, cols) in enumerate(((u23[0], chunks[2]), (u23[1], chunks[3]), (u01[0], chunks[0]), (u01[1], chunks[1]))):
            width = cols.stop - cols.start
            codes = pool.tile([P, width], U32, name="codes%d" % i, align_bytes=64)
            nc.vector.quantize_mx(
                out=codes[:].bitcast(FP8X4), scales=u_scales[:, cols], in_=u[:].rearrange("p n t -> p (n t)")
            )
            scores = psum.tile([P, width], F32, name=("scores0", "scores1", "scores2", "scores3")[i])
            nc.tensor.matmul_mx(
                out=scores[:],
                lhsT=q_codes[:].bitcast(FP8X4),
                lhsT_scale=q_scales[:],
                rhs=codes[:].bitcast(FP8X4),
                rhs_scale=u_scales[:, cols],
                start=True,
                stop=True,
            )
            scored.append((scores, cols))

        neg_x = pool.tile([P, N], F32, name="u1", align_bytes=64)
        for scores, cols in scored:
            nc.vector.tensor_tensor(neg_x[:, cols], neg_b[:, cols], scores[:], ALU.subtract)
        neg_m = pool.tile([P, 1], F32, name="neg_m")
        nc.vector.tensor_reduce(neg_m[:], neg_x[:], AX.X, ALU.min)
        e = pool.tile([P, N], F32, name="e")
        total = pool.tile([P, 1], F32, name="total")
        nc.scalar.activation(e[:], neg_x[:], ACT.Exp, bias=neg_m[:], scale=-1.0, accum_out=total[:])
        inv = pool.tile([P, 1], F32, name="inv")
        nc.vector.reciprocal(inv[:], total[:])
        y = pool.tile([P, N], F32, name="y", align_bytes=DMA_ALIGN)
        first, rest = slice(0, ON_SCALAR), slice(ON_SCALAR, N)
        nc.scalar.activation(y[:, first], e[:, first], ACT.Copy, scale=inv[:])
        nc.vector.tensor_scalar_mul(y[:, rest], e[:, rest], inv[:])
        nc.sync.dma_start(out[0], y[:])
